import numpy as np, ml_dtypes
CORES = [24,25,26,27,28,29,30,31]
N = 8
import mx_ref
BF = ml_dtypes.bfloat16
def gentries(a):
    return np.ascontiguousarray(a.reshape(8, 16, -1).transpose(0, 2, 1)).reshape(8, -1)
def gtable(e):
    e = np.asarray(e); return np.ascontiguousarray(e.reshape(8, -1, 16).transpose(0, 2, 1)).reshape(128, -1).astype(np.int32)
def gcols(t, e):
    v = np.concatenate([t.reshape(8, 16, -1, 4), np.zeros((8, 16, 1, 4), BF)], axis=2)
    return np.ascontiguousarray(np.stack([v[g][:, e[g]] for g in range(8)])).reshape(128, -1)
def tile(rs):
    return np.stack(rs, axis=2).reshape(128, -1).astype(BF)
def pick(q, e):
    c = np.concatenate([q[0].reshape(128, -1, 4), np.zeros((128, 1, 4), np.uint8)], axis=1); s = np.concatenate([q[1], np.ones((16, 1), np.uint8)], axis=1)
    return (np.ascontiguousarray(c[:, e].reshape(128, -1)), np.ascontiguousarray(s[:, e]))
def join(*qs):
    return (np.concatenate([q[0] for q in qs], axis=1), np.concatenate([q[1] for q in qs], axis=1))
def put(q, e, v):
    c, s = q[0].reshape(128, -1, 4).copy(), q[1].copy(); c[:, e] = v[0].reshape(128, -1, 4); s[:, e] = v[1]
    return (c.reshape(128, -1), s)
def pk(c, s):
    return (np.ascontiguousarray(c), mx_ref.live(s))
def emit(q):
    return q[0], q[1]
def packed(v, rng):
    q = [mx_ref.quantize(np.ascontiguousarray(v[r])) for r in range(N)]
    return np.stack([a for a, b in q]), np.stack([mx_ref.plane(b, rng) for a, b in q])
def values_of_codes():
    e, c = np.zeros((128, 128, 4), np.float32), np.zeros((128, 2, 4), np.uint8)
    e[np.arange(128), np.arange(128), 0] = 1
    c[:127, :, 0] = np.arange(256).reshape(2, 128).T[:127]
    return mx_ref.matmul(mx_ref.quantize(e.reshape(128, 512).astype(BF)), (c.reshape(128, 8), np.full((16, 2), 127, np.uint8))).T.reshape(-1).astype(np.float64)
CODE_VALUE, SCALE_VALUE = values_of_codes(), 2.0 ** (np.arange(256) - 127.0)
def decode(q):
    return (CODE_VALUE[q[0]].reshape(16, 8, -1, 4) * SCALE_VALUE[q[1]][:, None, :, None] + 0.0).reshape(128, -1).astype(np.float32)
def f(rng, *shape):
    return mx_ref.flush((rng.standard_normal(shape, dtype=np.float32) * np.exp2(rng.integers(-2, 3, shape[:-1] + (1,)))).astype(BF))
def wide(rng, *shape, cols=0):
    v = rng.standard_normal(shape, dtype=np.float32) * np.exp2(rng.integers(-12, 13, shape)).astype(np.float32)
    if cols: v *= np.repeat(np.exp2(rng.integers(-cols, cols + 1, shape[:-2] + (1, shape[-1] // 4))) * (rng.random(shape[:-2] + (1, shape[-1] // 4)) > 0.0625), 4, axis=-1).astype(np.float32)
    return mx_ref.flush(v.astype(BF))
C, M, R = 256, 128, 3
SH = (N, 8, 2, C, 4)
def numbers_of(rng):
    return {"x": np.array(f(rng, N, 128, 4 * C)), "u": np.array(f(rng, N, 128, 512)), "v": np.array(f(rng, N, 128, 512))}
def lists_of(e, c, a):
    return {"al": np.stack([gtable(e[r]) for r in range(N)]), "nx": np.stack([gtable((512 * c + a)[r].reshape(8, 8 * C)) for r in range(N)])}
def lists(rng):
    return lists_of(rng.integers(0, C, (N, 8, C)), rng.integers(0, 5, SH), rng.integers(0, C, SH))
def layers(rng, still=0):
    w = np.array(f(rng, N, 128, 2048)).reshape(N, 8, 16, 4, 8, 16, 4)
    w[:, :, :still] = 0
    w[:, :, :, :, :, :still] = 0
    return w
def weights(rng, w):
    c, s = packed(np.ascontiguousarray(w).reshape(N, 128, 2048), rng)
    return {"wc": c, "ws": s}
def setup_inputs(rng):
    return {**numbers_of(rng), **lists(rng), **weights(rng, layers(rng))}
def setup_inputs_near(rng):
    d = numbers_of(rng)
    x = d["x"].reshape(N, 8, 16, C, 4)
    u = d["u"].reshape(N, 128, 128, 4)
    o = rng.permutation(N) % 2
    x[:, :, :8] = 0
    u[:, :, ::16] = 0
    u[:, :, 1::16] = 0
    for r in range(N):
        k = 2.0 ** -30 if o[r] == 0 else 1.0
        s = rng.integers(-1, 2, (8, 2, C)) * k
        for g in rng.permutation(8)[:4]: s[g, :, rng.integers(C)] = 2.0 ** 14 * rng.choice([-1.0, 1.0], 2)
        x[r, :, :2, :, 0] = s.astype(np.float32).astype(BF)
        t = np.where(s[:, 0] == 0, rng.integers(-1, 2, (8, C)), 0) * k
        x[r, :, 2, :, 0] = (1.125 * t).astype(np.float32).astype(BF)
        x[r, :, 3, :, 0] = (-t).astype(np.float32).astype(BF)
        for h in [0, 16, 32, 48, 64, 80, 96, 112, 1, 17]:
            u[r, h, h, 0] = k
            u[r, h - h % 16 + 2, h, 0] = 1.125 * k
            u[r, h - h % 16 + 3, h, 0] = 1.25 * k
    return {"x": x.reshape(N, 128, 4 * C), "u": u.reshape(N, 128, 512), "v": d["v"], **lists(rng), **weights(rng, layers(rng, 8))}
def setup_inputs_chain(rng):
    d = numbers_of(rng)
    e = rng.permutation(N)
    c = rng.integers(0, 5, SH)
    i = np.arange(4)
    c[e[0]] = rng.integers(1, 5, SH[1:])
    c[e[1]] = 0
    c[e[2]] = np.where(np.arange(8)[:, None] <= 2 * i, i + 1, 0)[:, None, None, :]
    c[e[3]][:, 0] = 0
    c[e[3]][:, 1] = rng.integers(1, 5, (8, C, 4))
    return {**d, **lists_of(rng.integers(0, C, (N, 8, C)), c, rng.integers(0, C, SH)), **weights(rng, layers(rng))}
def setup_inputs_twice(rng):
    d = numbers_of(rng)
    s = 2.0 ** -rng.integers(8, 15, (N, 16, C, 32)) * (1.125 + 0.25 * rng.integers(0, 4, (N, 16, C, 32)))
    s[:, :, :, 4] = 2.0 ** -rng.integers(8, 12, (N, 16, C)) * (1.125 + 0.25 * rng.integers(0, 4, (N, 16, C)))
    np.put_along_axis(s, rng.integers(8, 32, (N, 16, C, 1)), 1.96875, axis=3)
    s = s * rng.choice([-1.0, 1.0], s.shape)
    s[:, :, :, 0] = 0.125 * s[:, :, :, 4]
    s = s * np.exp2(rng.integers(10, 13, (N, 16, C, 1)))
    x = np.ascontiguousarray(s.reshape(N, 16, C, 8, 4).transpose(0, 1, 3, 2, 4)).reshape(N, 128, 4 * C)
    u = d["u"].reshape(N, 128, 128, 4)
    u[:, :, ::16] = 0
    for h in range(0, 128, 16):
        u[:, h, h, 0] = 1.0
        u[:, h + 1, h, 0] = -0.125
    w = np.array(mx_ref.flush((layers(rng).astype(np.float32) * np.float32(2.0 ** -12)).astype(BF))).reshape(N, 128, 4, 128, 4)
    i = np.arange(128)
    for b in range(4): w[:, i, b, i, b] = -1.0
    return {"x": x.astype(np.float32).astype(BF), "u": u.reshape(N, 128, 512), "v": d["v"], **lists(rng), **weights(rng, w)}
def setup_inputs_ends(rng):
    d = numbers_of(rng)
    e = rng.permutation(N)
    x = d["x"].reshape(N, 8, 16, C, 4)
    u = d["u"].reshape(N, 128, 128, 4)
    v = d["v"].reshape(N, 128, 128, 4)
    t = np.clip(rng.integers(-C, 2 * C, (N, 8, C)), 0, C - 1)
    c = 4 * rng.integers(0, 2, SH)
    a = np.clip(rng.integers(-C, 2 * C, SH), 0, C - 1)
    t[e[0]], c[e[0]], a[e[0]] = C - 1, 4, C - 1
    t[e[1]], c[e[1]], a[e[1]] = 0, 0, 0
    u[:, :, ::16] = 0
    u[:, :, 1::16] = 0
    for i in range(N):
        r = e[i]
        s = rng.integers(-1, 2, (8, C)) * 1.0
        s[rng.permutation(8)[:2]] = rng.choice([-1.0, 1.0], (2, 1))
        s = s * (2.0 ** -30 if i % 2 else 2.0 ** 14)
        x[r, :, :8] = s[:, None, :, None].astype(np.float32).astype(BF)
        for h in [0, 16, 32, 48, 64, 80, 96, 112, 1, 17]: u[r, h - h % 16:h - h % 16 + 8, h] = 2.0 ** -30 if i % 2 else 2.0 ** 30
    x[e[0]] = (2.0 ** 14 * rng.choice([-1.0, 1.0], (C, 1))).astype(np.float32).astype(BF)
    u[e[0]] = (2.0 ** 30 * rng.choice([-1.0, 1.0], (128, 1))).astype(np.float32).astype(BF)
    v[e[0]] = (2.0 ** 30 * rng.choice([-1.0, 1.0], (128, 1))).astype(np.float32).astype(BF)
    w = layers(rng, 8)
    w[e[0]][:, 8:, :, :, 8:] = 8
    w[e[1]] = 0
    v = (np.where(v < 0, -1.0, 1.0) * np.where(rng.permutation(N) % 2, 2.0 ** -30, 2.0 ** 30)[:, None, None, None]).astype(np.float32).astype(BF)
    return {"x": x.reshape(N, 128, 4 * C), "u": u.reshape(N, 128, 512), "v": v.reshape(N, 128, 512), **lists_of(t, c, a), **weights(rng, w)}
def setup_inputs_spread(rng):
    d = setup_inputs(rng)
    d["x"] = mx_ref.flush((wide(rng, N, 128, 4 * C, cols=6).astype(np.float32) * np.float32(2.0 ** -7)).astype(BF))
    return d
def check_inputs(d):
    b = []
    for k, most in (("x", 2.0 ** 14), ("u", 2.0 ** 30), ("v", 2.0 ** 30)):
        a = np.abs(d[k].astype(np.float32))
        if not (np.isfinite(a).all() and ((a == 0) | (a >= 2.0 ** -30) & (a <= most)).all()): b.append("a value of " + k)
    if not ((d["al"] >= 0) & (d["al"] < C)).all(): b.append("an entry of al")
    if not ((d["nx"] >= 0) & (d["nx"] < 2560) & (d["nx"] % 512 < C)).all(): b.append("an entry of nx")
    none, least, most = [emit(mx_ref.quantize(np.full((128, 16), k, np.float32).astype(BF)))[1][0, 0] for k in (0.0, 2.0 ** -30, 2.0 ** 30)]
    for r in range(N):
        if ((d["wc"][r] == 0x7F) | (d["wc"][r] == 0xFF)).any(): b.append("wc: a code that is no number")
        s = mx_ref.live(d["ws"][r])
        if ((s != none) & ((s < least) | (s > most))).any(): b.append("ws: a scale out of range")
        w = np.abs(decode(pk(d["wc"][r], d["ws"][r])).astype(np.float64)).reshape(128, 512, 4)
        if not (np.sum(w, axis=(0, 2)) <= 2048).all(): b.append("a column of W adds up to more than 2048")
    return b
def reference(x, u, v, al, nx, wc, ws):
    qu = [mx_ref.quantize(u[r]) for r in range(N)]
    lay = [pk(wc[r], ws[r]) for r in range(N)]
    now = [x[r] for r in range(N)]
    ad = np.stack([gentries(al[r]) for r in range(N)])
    follow = [gentries(nx[r]) for r in range(N)]
    for t in range(R):
        made = []
        for r in range(N):
            q = mx_ref.quantize(now[r])
            s = mx_ref.matmul(qu[r], q)
            edge = 2 * (s[1] > 0) + (s[17] > 0)
            on = np.ones(C, bool)
            for g in range(8):
                bit = s[16 * g][ad[r, g]] > 0
                n = follow[r][g][4 * C * bit + 4 * ad[r, g] + edge]
                ad[r, g] = np.where(on, n % 512, ad[r, g])
                on = on & (n >= 512)
                edge = np.where(on, n // 512 - 1, 0)
            made.append(mx_ref.quantize(gcols(decode(q).astype(BF), ad[r])))
        ad[:, :, C - M:] = np.roll(ad[:, :, C - M:], 1, axis=0)
        for r in range(N):
            q = join(pick(made[r], np.arange(C - M)), pick(made[r - 1], np.arange(C - M, C)))
            own = decode(q)
            now[r] = tile([mx_ref.matmul(pick(lay[r], np.arange(128 * b, 128 * b + 128)), q) * np.float32(0.015625) + own[:, b::4] for b in range(4)])
    y, oa = np.zeros((N, 128, C), np.float32), np.zeros((N, 8, C), np.float32)
    oc, osc = np.zeros((N, 128, 4 * C), np.uint8), np.zeros((N, 16, C), np.uint8)
    for r in range(N):
        q = mx_ref.quantize(now[r])
        y[r] = mx_ref.matmul(mx_ref.quantize(v[r]), q)
        oa[r] = ad[r]
        oc[r], osc[r] = emit(q)
    return {"y": y, "oa": oa, "oc": oc, "osc": osc}

@@ -1,0 +1,403 @@
+from concourse.mybir import dt, AluOpType, AxisListType, ActivationFunctionType
+
+A = AluOpType
+AF = ActivationFunctionType
+R = 3
+SCRATCH = {}
+for _d, _l in (
+        ("int32", "nx4:512 ep:512 e8:128 ep2:256 pp:128 ai0:128 ai:128 n4i:512 sl:256 slt:256 ip:8 iph:8 iy:2 k0:64 pc:32 ei:128 am:16"),
+        ("float32", "p4:128 pr:256 pw:256 nw:2304 kf:64 cst:32 geo:32 ss:128 key:128 norm:16 c8:16 pg:256 pt:256 "
+                    "ek:128 dd:128 yi:16 amc:16 tmp:128 jk:128 wk:112 bg:288 bt:288 val:16 oaf:256 ys:256"),
+        ("bfloat16", "n4:512 nr:2048 i64:128 c64:128 et:2048 ut:512 vt:512 sb:256 nbf:256 at:256 f:1024 fa:1024 "
+                     "co0:16 co1:16 ca0:16 ca1:16 xl0:512 xl1:512 xl2:512 xl3:512 xh0:512 xh1:512 xh2:512 xh3:512 "
+                     "zl0:512 zl1:512 zl2:512 zh0:512 zh1:512 zh2:512"),
+        ("uint16", "ul:8 lb:18 ou:16 nu:256 ga0:8 ga1:8 ga2:8 gl0:16 gl1:16 gl2:16")):
+    for _s in _l.split():
+        SCRATCH[_s.split(":")[0]] = ("sbuf", [128, int(_s.split(":")[1])], _d)
+for _s in "qe:512 lw:512 qu:128 qy:128 qv:128 qx:256:4 qh:128:3 ql:128:3 qn:256:3".split():
+    _p = _s.split(":")
+    for _t in ([""] if len(_p) == 2 else ["%d" % k for k in range(int(_p[2]))]):
+        SCRATCH[_p[0] + _t] = ("sbuf", [128, int(_p[1])], "float8_e4m3fn_x4")
+        SCRATCH[_p[0] + "s" + _t] = ("sbuf", [128, int(_p[1])], "uint8")
+BANK = ["b%d" % k for k in range(10, 18)]
+for _s in BANK:
+    SCRATCH[_s] = ("psum", [128, 512], "float32")
+SEMAPHORES = ("cv cs ct cg dnx dal dx du dv dw dpr dnr dyl dyh doa docl doch dgl0 dgl1 dgl2".split()
+              + [n + "%d" % t for n in ("rl", "ll", "rc", "lc", "rs", "ls", "rg", "lg") for t in range(R)])
+
+
+def rank_program(g, core, T, topo):
+    rank = T.rank_of(core)
+    if rank is None:
+        return
+    nxt = T.cores[(rank + 1) % len(T.cores)]
+    rid, pid, _ = topo.addr(nxt)
+    mask, neng = topo.mask(core, nxt), len(topo.engines(core, nxt))
+    V, S, P = g.vector, g.scalar, g.tensor
+    eng = {"v": V, "s": S, "t": P, "g": g, "y": g.sync}
+    csem = {"v": "cv", "s": "cs", "t": "ct", "g": "cg"}
+    cnt, wr, rd = {}, {}, {}
+    known = {q: {} for q in eng}
+
+    def deps(q, r, w):
+        toks = [wr[k] for k in r if k in wr]
+        for k in w:
+            toks += rd.get(k, []) + ([wr[k]] if k in wr else [])
+        toks = [t for t in toks if known[q].get(t[0], 0) < t[1]]
+        best = {}
+        for t in toks:
+            if t[0] not in best or best[t[0]][1] < t[1]:
+                best[t[0]] = t
+        for t in list(best.values()):
+            if not any(o is not t and o[2].get(t[0], 0) >= t[1] for o in best.values()):
+                eng[q].wait_ge(T.sem[t[0]], t[1])
+        for t in toks:
+            for s, n in list(t[2].items()) + [(t[0], t[1])]:
+                known[q][s] = max(known[q].get(s, 0), n)
+
+    def note(tok, r, w):
+        for k in r:
+            rd.setdefault(k, []).append(tok)
+        for k in w:
+            wr[k] = tok
+            rd[k] = []
+
+    def op(q, fn, r, w, more=""):
+        r, w = r.split(), w.split()
+        w = w + [k for k in r if k in BANK]
+        deps(q, r, w)
+        s = csem[q]
+        cnt[s] = cnt.get(s, 0) + 1
+        fn().then_inc(T.sem[s], 1)
+        clk = dict(known[q])
+        clk[s] = cnt[s]
+        note((s, cnt[s], clk), r, w + more.split())
+
+    def dmas(sem, lst, r, w):
+        r, w = r.split(), w.split()
+        qs = sorted(set(q for q, _, _ in lst))
+        for q in qs:
+            deps(q, r, w)
+        for q, o, i in lst:
+            cnt[sem] = cnt.get(sem, 0) + 16
+            eng[q].dma_start(o, i).then_inc(T.sem[sem], 16)
+        clk = {sem: cnt[sem]}
+        for q in qs:
+            for s, n in known[q].items():
+                clk[s] = max(clk.get(s, 0), n)
+        note((sem, cnt[sem], clk), r, w)
+
+    def send(out, inp, k, t, r, lands):
+        rs, ls, r = "r%s%d" % (k, t), "l%s%d" % (k, t), r.split()
+        deps("g", r, [])
+        g.remote_dma(out, inp, T.sem[rs], T.sem[ls], pid, rid, mask)
+        for s in (ls, rs):
+            cnt[s] = cnt.get(s, 0) + neng
+        note((ls, cnt[ls], {}), r, [])
+        note((rs, cnt[rs], {}), [], [lands])
+
+    def vs(out, i, s1, s2, o1, r, w, o2=None):
+        if o2 is None:
+            op("v", lambda: V.tensor_scalar(out, i, s1, None, o1), r, w)
+        else:
+            op("v", lambda: V.tensor_scalar(out, i, s1, s2, o1, o2), r, w)
+
+    def vt(out, a, b, o, r, w):
+        op("v", lambda: V.tensor_tensor(out, a, b, o), r, w)
+
+    def vc(out, i, r, w):
+        op("v", lambda: V.tensor_copy(out, i), r, w)
+
+    def ac(out, i, r, w, scale=None):
+        if scale is None:
+            op("s", lambda: S.activation(out, i, AF.Copy), r, w)
+        else:
+            op("s", lambda: S.activation(out, i, AF.Copy, scale=scale), r, w)
+
+    def fill(ap, c, w):
+        op("v", lambda: V.memset(ap, c), "", w)
+
+    def quant(o, s, i, r, w):
+        op("v", lambda: V.quantize_mx(o, s, i), r, w)
+
+    def turn(o, i, r, w):
+        op("v", lambda: V.transpose(o, i), r, w)
+
+    def scan(o, d, first, r, w):
+        op("v", lambda: V.tensor_tensor_scan(o, d, T.cst[:, 16:24], first, A.mult, A.add), r, w)
+
+    def iota(o, pat, base, cm, w, small=False):
+        if small:
+            op("g", lambda: g.iota(o, pat, base, cm, allow_small_or_imprecise_dtypes=True), "", w)
+        else:
+            op("g", lambda: g.iota(o, pat, base, cm), "", w)
+
+    def mm(bank, n, l, ls, rh, rs, r, start=True, stop=True):
+        op("t", lambda: P.matmul_mx(T[bank][:, 0:n], l, ls, rh, rs, start, stop), r, bank if start else "", bank)
+
+    k0, kf, wk = T.k0, T.kf, T.wk
+    dmas("dnx", [("ys"[e // 2], T.nx4[0:32, 128 * e:128 * e + 128], T.nx[e:128:4, :]) for e in range(4)], "", "nx4")
+    dmas("dx", [("y", T.xl0[:], T.x[:, 0:512]), ("s", T.xh0[:], T.x[:, 512:1024])], "", "xl0 xh0")
+    dmas("du", [("y", T.ut[:], T.u[:])], "", "ut")
+    fill(T.sl[:], 0, "sl")
+    fill(T.c64[:], 64.0, "c64")
+    dmas("dal", [("sy"[k % 2], T.sl[2 * k:128:16, 32 * k:32 * k + 32], T.al[16 * k:16 * k + 16, :]) for k in range(8)], "", "sl")
+    dmas("dw", [("y", T.lw[:].bitcast(dt.uint8), T.wc[:]), ("s", T.lws[:], T.ws[:])], "", "lw")
+    dmas("dv", [("y", T.vt[:], T.v[:])], "", "vt")
+
+    iota(T.ip[:], [[0, 8]], 0, 1, "ip")
+    iota(T.ai0[0:32, :], [[0, 2], [4, 64]], 0, 0, "ai0")
+    iota(T.iph[:], [[1, 8]], 0, 1, "iph")
+    iota(T.iy[:], [[2, 2]], 0, 16, "iy")
+    op("g", lambda: g.affine_select(T.i64[:], T.c64[:], [[-1, 128]], A.is_equal, 0.0, 0, 1), "c64", "i64")
+    iota(T.c8[:], [[0, 8], [64, 2]], -19, 0, "c8i", True)
+    iota(T.et[:], [[0, 2048]], 0, 0, "et", True)
+    for e in range(4):
+        iota(T.key[:, 32 * e:32 * e + 16], [[0, 8], [512, 2]], -31 - 32 * e, 0, "key%d" % e, True)
+        iota(T.key[:, 32 * e + 16:32 * e + 32], [[0, 8], [-512, 2]], 33 + 32 * e, 0, "key%d" % (e + 4), True)
+
+    fill(T.cst[:, 0:8], 2.0 ** -5, "cst0")
+    fill(T.cst[:, 8:16], 32.0, "cst1")
+    fill(T.cst[:, 16:24], 0.0, "cst2")
+    vs(k0[:, 0:1], T.ip[:, 0:1], 3, None, A.bitwise_and, "ip", "k0a")
+    scan(T.geo[:, 0:8], T.cst[:, 0:8], 64.0, "cst0 cst2", "geo0")
+    scan(T.geo[:, 8:16], T.cst[:, 8:16], 2.0 ** -9, "cst1 cst2", "geo1")
+    vc(kf[:, 0:1], k0[:, 0:1], "k0a", "kfa")
+    vs(k0[:, 8:16], T.ip[:], 14, None, A.bitwise_and, "ip", "k0b")
+    for y in range(2):
+        vc(T.ss[:, y:16:2], T.geo[:, 0:8], "geo0", "ss%d" % y)
+    vs(k0[:, 24:32], T.iph[:], 1, None, A.bitwise_and, "iph", "k0c")
+    vs(kf[:, 8:16], k0[:, 8:16], 8.0, None, A.mult, "k0b", "kfb")
+    vs(T.ai[0:32, :], T.ai0[0:32, :], kf[0:32, 0:1], 65536.0, A.add, "ai0 kfa", "aix", A.mult)
+    vc(T.ss[:, 16:32], T.ss[:, 0:16], "ss0 ss1", "ss2")
+    vt(kf[:, 16:24], kf[:, 8:16], k0[:, 24:32], A.add, "kfb k0c", "kfc")
+    vs(T.ai[0:32, :], T.ai[0:32, :], 7 * 4369.0, None, A.add, "aix", "ai")
+    vc(T.ss[:, 32:64], T.ss[:, 0:32], "ss0 ss1 ss2", "ss3")
+    vc(T.ul[:], kf[:, 16:24], "kfc", "ul")
+
+    vs(T.e8[0:32, :], T.nx4[0:32, 384:512], 8.0, None, A.mult, "nx4", "e8")
+    for e in range(4):
+        a = slice(128 * e, 128 * e + 128)
+        if e < 3:
+            vs(T.ep[0:32, a], T.nx4[0:32, a], 9 - 4 * e, 7 << (4 * e), A.logical_shift_right, "nx4", "ep%d" % e, A.bitwise_and)
+        else:
+            vs(T.ep[0:32, a], T.e8[0:32, :], 7 << 12, None, A.bitwise_and, "e8", "ep3")
+    vt(T.ep2[0:32, :], T.ep[0:32, 0:256], T.ep[0:32, 256:512], A.add, "ep0 ep1 ep2 ep3", "epx")
+    vt(T.pp[0:32, :], T.ep2[0:32, 0:128], T.ep2[0:32, 128:256], A.add, "epx", "pp")
+    vt(T.p4[0:32, :], T.pp[0:32, :], T.ai[0:32, :], A.add, "pp ai", "p4")
+    lst = []
+    for H in range(8):
+        for b in range(2):
+            z = (b + H) % 2
+            lst.append(("sy"[b], T.pr[16 * H + z:16 * H + 16:2, :], T.p4[0:32, 64 * b:64 * b + 64]))
+    dmas("dpr", lst, "p4", "pr")
+    vs(T.n4i[0:32, :], T.nx4[0:32, :], 511, None, A.bitwise_and, "nx4", "n4i")
+    vc(T.n4[0:32, :], T.n4i[0:32, :], "n4i", "n4")
+    dmas("dnr", [("sy"[z], T.nr[16 * H + z:16 * H + 16:2, :], T.n4[0:32, :]) for H in range(8) for z in range(2)], "n4", "nr")
+    for b in range(4):
+        ac(T.et[:, 512 * b + b:512 * b + 512:4], T.i64[:], "i64 et", "et_%d" % b)
+
+    def score_mm(t, h):
+        a = slice(128 * h, 128 * h + 128)
+        mm(BANK[h], 128, T.qy[:], T.qys[:], T["qx%d" % t][:, a], T["qxs%d" % t][:, a], "qy qys qx%d" % t + "LH"[h])
+
+    def score_bits(h):
+        vs(T.sb[:, 128 * h:128 * h + 128], T[BANK[h]][:, 0:128], 0.0, 0.5, A.is_gt, BANK[h], "sb%d" % h, A.subtract)
+
+    def send_state(t):
+        k = "qx%dL qx%dH" % (t, t)
+        send(T["qn%d" % t][:].bitcast(dt.uint8), T["qx%d" % t][:].bitcast(dt.uint8), "c", t, k, "qnc%d" % t)
+        send(T["qns%d" % t][:], T["qxs%d" % t][:], "s", t, k, "qns%d" % t)
+
+    quant(T.qu[:], T.qus[:], T.ut[:], "ut", "qu")
+    turn(T.slt[:], T.sl[:], "sl", "slt")
+    vc(T.qy[:].bitcast(dt.uint32), T.qu[:].bitcast(dt.uint32).indirect(T.ul[:]), "qu ul", "qy")
+    ac(T.qys[:], T.qus[:].indirect(T.ul[:]), "qu ul", "qys")
+    quant(T.qx0[:, 0:128], T.qxs0[:, 0:128], T.xl0[:], "xl0", "qx0L")
+    quant(T.qx0[:, 128:256], T.qxs0[:, 128:256], T.xh0[:], "xh0", "qx0H")
+    iota(T.nw[:, 2048:2304], [[1, 256]], 0, 0, "nwi", True)
+    send_state(0)
+    score_mm(0, 0)
+    score_mm(0, 1)
+    vs(k0[:, 32:34], T.ip[:, 0:2], 4, None, A.logical_shift_right, "ip", "k0e")
+    vc(T.lb[:, 0:16:2], T.slt[:, 0:256:34], "slt", "lb0")
+    vc(T.lb[:, 1:16:2], T.slt[:, 16:256:34], "slt", "lb1")
+    vs(k0[:, 16:17], k0[:, 32:33], 1, None, A.bitwise_and, "k0e", "k0d")
+    vs(kf[:, 32:34], k0[:, 32:34], -254.0, None, A.mult, "k0e", "kfe")
+    vs(T.c8[:], T.c8[:], 0.5, None, A.mult, "c8i", "c8")
+    vc(kf[:, 40:41], k0[:, 16:17], "k0d", "kfd")
+    vt(kf[:, 34:36], kf[:, 32:34], T.iy[:], A.add, "kfe iy", "kff")
+    vc(T.ss[:, 64:128], T.ss[:, 0:64], "ss0 ss1 ss2 ss3", "ss4")
+    vs(T.lb[:, 16:18], kf[:, 34:36], kf[:, 40:41], None, A.subtract, "kff kfd", "lbj")
+    score_bits(0)
+    score_bits(1)
+    vc(T.norm[:, 0:16:2], T.geo[:, 8:16], "geo1", "norm0")
+    vs(T.norm[:, 1:16:2], T.geo[:, 8:16], -1.0, None, A.mult, "geo1", "norm1")
+    for r in range(4):
+        (ac if r % 2 else vc)(T.pw[:, r:256:4], T.pr[:, 64 * r:64 * r + 64], "pr", "pw%d" % r)
+
+    def prefetch_pick():
+        ac(T.pg[:], T.pw[:].indirect(T.lb[:, 0:16]), "pw0 pw1 pw2 pw3 lb0 lb1", "pg")
+
+    def prefetch_1():
+        turn(T.pt[:], T.pg[:], "pg", "pt")
+        vc(T.pc[:, 0:16], T.pt[:, 0:256:17], "pt", "pc0")
+        vc(T.pc[:, 16:32:2], T.pt[:, 1:256:34], "pt", "pc1")
+        vc(T.pc[:, 17:32:2], T.pt[:, 16:256:34], "pt", "pc2")
+
+    def prefetch_2():
+        vs(T.am[:], T.pc[:, 0:16], 16, None, A.logical_shift_right, "pc0", "am")
+        for e in range(4):
+            vs(T.ei[:, 32 * e:32 * e + 32], T.pc[:], 4 * e, 7, A.logical_shift_right, "pc0 pc1 pc2", "ei%d" % e, A.bitwise_and)
+        vs(T.yi[:], T.am[:], 2.0 ** -8, 8.0, A.mult, "am", "yi", A.add)
+        vt(T.ek[:], T.ei[:], T.key[:], A.add, "ei0 ei1 ei2 ei3 " + " ".join("key%d" % k for k in range(8)), "ek")
+        vt(T.amc[:], T.yi[:], T.c8[:], A.add, "yi c8", "amc")
+        vt(T.dd[:], T.ek[:], T.ss[:], A.mult, "ek ss0 ss1 ss2 ss3 ss4", "dd")
+
+    def bits_pick():
+        ac(T.bg[:, 160:288], T.sb[:].indirect(T.lb[:, 10:18]), "sb0 sb1 lb0 lb1 lbj", "bg1")
+        vc(T.bg[:, 0:160], T.sb[:].indirect(T.lb[:, 0:10]), "sb0 sb1 lb0 lb1", "bg0")
+
+    prefetch_pick()
+    bits_pick()
+    quant(T.qe[:], T.qes[:], T.et[:], "et et_0 et_1 et_2 et_3", "qe")
+    for r in range(4):
+        ac(T.nw[:, r:2048:4], T.nr[:, 512 * r:512 * r + 512], "nr", "nw%d" % r)
+    NW = "nw0 nw1 nw2 nw3 nwi "
+    prefetch_1()
+    prefetch_2()
+
+    bt, val, tmp = T.bt, T.val, T.tmp
+    for t in range(R):
+        ts = "%d" % t
+        gl, ga = T["gl" + ts], T["ga" + ts]
+        halves = (("f", T.f, [2, 3, 4, 5], "qx", "qx%dL qx%dH" % (t, t)), ("fa", T.fa, [6, 7, 0, 1], "qn", "qnc%d qns%d" % (t, t)))
+        if t:
+            bits_pick()
+        for _, _, bk, q, k in halves:
+            for b in range(4):
+                a = slice(128 * b, 128 * b + 128)
+                mm(BANK[bk[b]], 256, T.qe[:, a], T.qes[:, a], T[q + ts][:], T[q + "s" + ts][:], "qe " + k)
+        turn(bt[:, 256:288], T.bg[:, 256:288], "bg1", "bte")
+        vs(wk[:, 0:1], bt[:, 257:258], 64.0, 80.0, A.mult, "bte", "w0", A.add)
+        op("s", lambda: S.activation(wk[:, 8:9], bt[:, 272:273], AF.Identity, bias=432.0, scale=-64.0), "bte", "w1")
+        turn(bt[:, 0:256], T.bg[:, 0:256], "bg0 bg1", "bt")
+        vs(val[:, 0:1], bt[:, 259:260], 32.0, wk[:, 0:1], A.mult, "bte w0", "val0", A.add)
+        op("s", lambda: S.activation(val[:, 1:2], bt[:, 274:275], AF.Identity, bias=wk[:, 8:9], scale=-32.0), "bte w1", "val1")
+        x0, x1, x2, o = wk[:, 32:46], wk[:, 48:62], wk[:, 64:78], T.ou
+
+        def last(y):
+            i = 14 + y
+            vs(wk[:, 46 + y:47 + y], val[:, i:i + 1], (-1.0) ** y * 2.0 ** 31, wk[:, 16 + i:17 + i], A.mult, "val%d b3" % i, "l%d" % y, A.add)
+
+        def last2(y):
+            i = 14 + y
+            vs(o[:, i:i + 1], wk[:, 46 + y:47 + y], T.yi[:, i:i + 1], 256.0, A.min, "l%d yi" % y, "ou%d" % y, A.mult)
+
+        for i in range(14):
+            c, d = slice(8 * i, 8 * i + 8), T.dd[:, i:128:16]
+            me, sg, new = val[:, i:i + 1], bt[:, 17 * i:17 * i + 1], val[:, i + 2:i + 3]
+            if i % 2:
+                op("s", lambda: S.activation(tmp[:, c], d, AF.Abs, bias=me, scale=sg), "dd bt val%d" % i, "tmp%d" % i)
+                op("s", lambda: S.activation(T.jk[:, c], tmp[:, c], AF.Relu, bias=16.0 * 32.0 ** -(i // 2), scale=-1.0, accum_out=new),
+                   "tmp%d" % i, "jk%d val%d" % (i, i + 2))
+            else:
+                vs(tmp[:, c], d, sg, me, A.mult, "dd bt val%d" % i, "tmp%d" % i, A.subtract)
+                if i == 2:
+                    vt(wk[:, 16:32], bt[:, 0:256:17], T.amc[:], A.add, "bt amc", "b3")
+                op("v", lambda: V.tensor_reduce(new, tmp[:, c], AxisListType.X, A.min, apply_absolute_value=True), "tmp%d" % i, "val%d" % (i + 2))
+        vt(x0, val[:, 0:14], T.norm[:, 0:14], A.mult, "norm0 norm1 " + " ".join("val%d" % i for i in range(14)), "t1")
+        last(0)
+        vt(x1, x0, wk[:, 16:30], A.add, "t1 b3", "t2")
+        last2(0)
+        vt(x2, x1, T.yi[:, 0:14], A.min, "t2 yi", "t3")
+        last(1)
+        vs(o[:, 0:14], x2, 256.0, None, A.mult, "t3", "ou")
+        last2(1)
+        vc(T.nu[:], T.nw[:].indirect(o[:]), NW + "ou ou0 ou1", "nu")
+        if t < R - 1:
+            ac(T.nbf[:], T.nw[:].indirect(o[:]), NW + "ou ou0 ou1", "nbf")
+        dmas("dgl" + ts, [("ys"[k % 2], gl[16 * k:16 * k + 16, :], T.nu[2 * k:128:16, 32 * k:32 * k + 32]) for k in range(8)], "nu", "gl" + ts)
+        if t < R - 1:
+            co = T["co" + ts]
+            turn(T.at[:], T.nbf[:], "nbf", "at")
+            vc(co[:], T.at[:, 0:256:17], "at", "co" + ts)
+            send(T["ca" + ts][:], co[:], "l", t, "co" + ts, "ca" + ts)
+        send(ga[:], gl[:, 8:16], "g", t, "gl" + ts, "ga" + ts)
+        for n, f, bk, _, _ in halves:
+            for b in range(4):
+                bank = BANK[bk[b]]
+                fo, fi = f[:, 256 * b:256 * b + 256], T[bank][:, 0:256]
+                if b % 2:
+                    vs(fo, fi, 0.015625, None, A.mult, bank, "%s_%d" % (n, b))
+                else:
+                    ac(fo, fi, bank, "%s_%d" % (n, b), 0.015625)
+            if n == "f" and t < R - 1:
+                if t == 0:
+                    vs(k0[:, 40:41], T.ip[:, 0:1], 8, None, A.bitwise_and, "ip", "k0m")
+                    vs(kf[:, 56:57], k0[:, 40:41], 0.0, None, A.is_equal, "k0m", "mlo")
+                    vs(kf[:, 57:58], k0[:, 40:41], 0.0, None, A.is_gt, "k0m", "mhi")
+                vs(wk[:, 80:96], co[:], kf[:, 56:57], None, A.mult, "mlo co" + ts, "m1")
+
+        def make_z(h):
+            k, n, off, ok = "lh"[h] + ts, ("f", "fa")[h], (gl[:, 0:8], ga[:])[h], ("gl", "ga")[h] + ts
+            z = T["z" + k]
+            for b in range(4):
+                (vc if b < 2 else ac)(z[:, b:512:4], T[n][:, 256 * b:256 * b + 256].indirect(off), "%s_%d %s" % (n, b, ok), "z%s_%d" % (k, b))
+            quant(T["q" + k][:], T["q" + "lh"[h] + "s" + ts][:], z[:], " ".join("z%s_%d" % (k, b) for b in range(4)), "q" + k)
+
+        def make_r(h):
+            q, qs, kk = T["q" + "lh"[h] + ts], T["q" + "lh"[h] + "s" + ts], "q" + "lh"[h] + ts
+            for b in range(4):
+                a = slice(128 * b, 128 * b + 128)
+                mm(BANK[4 * h + b], 128, T.lw[:, a], T.lws[:, a], q[:], qs[:], "lw " + kk, True, False)
+                mm(BANK[4 * h + b], 128, T.qe[:, a], T.qes[:, a], q[:], qs[:], "qe " + kk, False, True)
+
+        def make_x(h):
+            a, xk = slice(128 * h, 128 * h + 128), "x%s%d" % ("lh"[h], t + 1)
+            for b in range(4):
+                bank = BANK[4 * h + b]
+                xo, xi, w = T[xk][:, b:512:4], T[bank][:, 0:128], "%s_%d" % (xk, b)
+                if b % 2:
+                    vs(xo, xi, 0.015625, None, A.mult, bank, w)
+                else:
+                    ac(xo, xi, bank, w, 0.015625)
+            qn, qns, key = T["qx%d" % (t + 1)], T["qxs%d" % (t + 1)], "qx%d%s" % (t + 1, "LH"[h])
+            quant(qn[:, a], qns[:, a], T[xk][:], " ".join("%s_%d" % (xk, b) for b in range(4)), key)
+            if t < R - 1:
+                score_mm(t + 1, h)
+                return
+            mm(BANK[h], 128, T.qv[:], T.qvs[:], qn[:, a], qns[:, a], "qv " + key)
+            lst = [("y", T.oc[:, 512 * h:512 * h + 512], qn[:, a].bitcast(dt.uint8))]
+            lst += [("y", T.osc[4 * k:4 * k + 4, a], qns[32 * k:32 * k + 4, a]) for k in range(4)]
+            dmas("doc" + "lh"[h], lst, key, "")
+            ac(T.oaf[:, a], T.nw[:, 2048:2304].indirect(ga[:] if h else gl[:, 0:8]), "nwi " + ("ga" if h else "gl") + ts, "oa%d" % h)
+            ac(T.ys[:, a], T[BANK[h]][:, 0:128], BANK[h], "ys%d" % h)
+            dmas("dy" + "lh"[h], [("s", T.y[:, a], T.ys[:, a])], "ys%d" % h, "")
+
+        make_z(0)
+        make_r(0)
+        if t < R - 1:
+            vs(wk[:, 96:112], T["ca" + ts][:], kf[:, 57:58], None, A.mult, "mhi ca" + ts, "m2")
+            vt(wk[:, 32:48], wk[:, 80:96], wk[:, 96:112], A.add, "m1 m2", "t1 l0 l1")
+            vc(T.lb[:, 0:16], wk[:, 32:48], "t1", "lb0 lb1")
+            prefetch_pick()
+            make_x(0)
+            prefetch_1()
+            make_z(1)
+            make_r(1)
+            score_bits(0)
+            prefetch_2()
+            make_x(1)
+            send_state(t + 1)
+            score_bits(1)
+        else:
+            quant(T.qv[:], T.qvs[:], T.vt[:], "vt", "qv")
+            make_x(0)
+            make_z(1)
+            make_r(1)
+            make_x(1)
+    dmas("doa", [("y", T.oa[:], T.oaf[0:128:16, :])], "oa0 oa1", "")
+    for s in sorted(cnt):
+        if known["g"].get(s, 0) < cnt[s]:
+            g.wait_ge(T.sem[s], cnt[s])

@@ -1,19 +1,21 @@
-from concourse.mybir import dt, AluOpType, AxisListType, ActivationFunctionType
+from concourse.mybir import dt, AluOpType, ActivationFunctionType
 
 A = AluOpType
 AF = ActivationFunctionType
 R = 3
+L = 21
+BIG = 1.5 * 2.0 ** 23
 SCRATCH = {}
 for _d, _l in (
-        ("int32", "nx4:512 ep:512 e8:128 ep2:256 pp:128 ai0:128 ai:128 n4i:512 sl:256 slt:256 ip:8 iph:8 iy:2 k0:64 pc:32 ei:128 am:16"),
-        ("float32", "p4:128 pr:256 pw:256 nw:2304 kf:64 cst:32 geo:32 ss:128 key:128 norm:16 c8:16 pg:256 pt:256 "
-                    "ek:128 dd:128 yi:16 amc:16 tmp:128 jk:128 wk:112 bg:288 bt:288 val:16 oaf:256 ys:256"),
-        ("bfloat16", "n4:512 nr:2048 i64:128 c64:128 et:2048 ut:512 vt:512 sb:256 nbf:256 at:256 f:1024 fa:1024 "
-                     "co0:16 co1:16 ca0:16 ca1:16 xl0:512 xl1:512 xl2:512 xl3:512 xh0:512 xh1:512 xh2:512 xh3:512 "
+        ("int32", "nxi:128 nt:128 ali:16 i16:8"),
+        ("float32", "uu:16,5,16 tab:256 cs:8,16 ct:8,16 jj:176 d1:360 ini:176 oo:6,105 pg:256 gm:256 tb:256 "
+                    "t1:4,16 t2:2,2,16 t3:64 idt:256 oaf:256 ys:256"),
+        ("bfloat16", "i64:128 c64:128 et:2048 ut:512 vt:512 sb:256 eg:256 f:1024 fa:1024 "
+                     "xl0:512 xl1:512 xl2:512 xl3:512 xh0:512 xh1:512 xh2:512 xh3:512 "
                      "zl0:512 zl1:512 zl2:512 zh0:512 zh1:512 zh2:512"),
-        ("uint16", "ul:8 lb:18 ou:16 nu:256 ga0:8 ga1:8 ga2:8 gl0:16 gl1:16 gl2:16")):
+        ("uint16", "ul:8 g0:16 gl0:8 gl1:8 gl2:8 go0:8 go1:8 go2:8 ga0:8 ga1:8 ga2:8")):
     for _s in _l.split():
-        SCRATCH[_s.split(":")[0]] = ("sbuf", [128, int(_s.split(":")[1])], _d)
+        SCRATCH[_s.split(":")[0]] = ("sbuf", [128] + [int(k) for k in _s.split(":")[1].split(",")], _d)
 for _s in "qe:512 lw:512 qu:128 qy:128 qv:128 qx:256:4 qh:128:3 ql:128:3 qn:256:3".split():
     _p = _s.split(":")
     for _t in ([""] if len(_p) == 2 else ["%d" % k for k in range(int(_p[2]))]):
@@ -22,8 +24,8 @@ for _s in "qe:512 lw:512 qu:128 qy:128 qv:128 qx:256:4 qh:128:3 ql:128:3 qn:256:
 BANK = ["b%d" % k for k in range(10, 18)]
 for _s in BANK:
     SCRATCH[_s] = ("psum", [128, 512], "float32")
-SEMAPHORES = ("cv cs ct cg dnx dal dx du dv dw dpr dnr dyl dyh doa docl doch dgl0 dgl1 dgl2".split()
-              + [n + "%d" % t for n in ("rl", "ll", "rc", "lc", "rs", "ls", "rg", "lg") for t in range(R)])
+SEMAPHORES = ("cv cs ct cg dnx dal dxl dxh du dv dw dyl dyh doa docl doch".split()
+              + [n + "%d" % t for n in ("rc", "lc", "rs", "ls", "rg", "lg") for t in range(R)])
 
 
 def rank_program(g, core, T, topo):
@@ -65,6 +67,7 @@ def rank_program(g, core, T, topo):
     def op(q, fn, r, w, more=""):
         r, w = r.split(), w.split()
         w = w + [k for k in r if k in BANK]
+        w = w + ["pool"] * (q == "g")
         deps(q, r, w)
         s = csem[q]
         cnt[s] = cnt.get(s, 0) + 1
@@ -123,238 +126,176 @@ def rank_program(g, core, T, topo):
     def turn(o, i, r, w):
         op("v", lambda: V.transpose(o, i), r, w)
 
-    def scan(o, d, first, r, w):
-        op("v", lambda: V.tensor_tensor_scan(o, d, T.cst[:, 16:24], first, A.mult, A.add), r, w)
+    def scan(o, d0, d1, r, w):
+        op("v", lambda: V.tensor_tensor_scan(o, d0, d1, 0.0, A.mult, A.add), r, w)
 
-    def iota(o, pat, base, cm, w, small=False):
-        if small:
-            op("g", lambda: g.iota(o, pat, base, cm, allow_small_or_imprecise_dtypes=True), "", w)
-        else:
-            op("g", lambda: g.iota(o, pat, base, cm), "", w)
+    def iota(o, pat, base, cm, w, r=""):
+        op("g", lambda: g.iota(o, pat, base, cm, allow_small_or_imprecise_dtypes=True), r, w)
 
     def mm(bank, n, l, ls, rh, rs, r, start=True, stop=True):
         op("t", lambda: P.matmul_mx(T[bank][:, 0:n], l, ls, rh, rs, start, stop), r, bank if start else "", bank)
 
-    k0, kf, wk = T.k0, T.kf, T.wk
-    dmas("dnx", [("ys"[e // 2], T.nx4[0:32, 128 * e:128 * e + 128], T.nx[e:128:4, :]) for e in range(4)], "", "nx4")
-    dmas("dx", [("y", T.xl0[:], T.x[:, 0:512]), ("s", T.xh0[:], T.x[:, 512:1024])], "", "xl0 xh0")
-    dmas("du", [("y", T.ut[:], T.u[:])], "", "ut")
-    fill(T.sl[:], 0, "sl")
-    fill(T.c64[:], 64.0, "c64")
-    dmas("dal", [("sy"[k % 2], T.sl[2 * k:128:16, 32 * k:32 * k + 32], T.al[16 * k:16 * k + 16, :]) for k in range(8)], "", "sl")
-    dmas("dw", [("y", T.lw[:].bitcast(dt.uint8), T.wc[:]), ("s", T.lws[:], T.ws[:])], "", "lw")
+    def half(h):
+        return slice(128 * h, 128 * h + 128)
+
+    def quad(q):
+        return slice(32 * q, 32 * q + 32)
+
+    uu, cs, d1, oo = T.uu, T.cs, T.d1, T.oo
+    thr, bit, mul, scl = [T.ct[:, 2 * k, 0:1] for k in range(4)]
+    dmas("dnx", [("y", T.nxi[:], T.nx[:])], "", "nxi")
+    dmas("du", [("s", T.ut[:], T.u[:])], "", "ut")
+    dmas("dxl", [("y", T.xl0[:], T.x[:, 0:512])], "", "xl0")
+    dmas("dxh", [("s", T.xh0[:], T.x[:, 512:1024])], "", "xh0")
+    dmas("dal", [("y", T.ali[:], T.al[:])], "", "ali")
+    dmas("dw", [("y", T.lw[:].bitcast(dt.uint8), T.wc[:]), ("y", T.lws[:], T.ws[:])], "", "lw")
     dmas("dv", [("y", T.vt[:], T.v[:])], "", "vt")
 
-    iota(T.ip[:], [[0, 8]], 0, 1, "ip")
-    iota(T.ai0[0:32, :], [[0, 2], [4, 64]], 0, 0, "ai0")
-    iota(T.iph[:], [[1, 8]], 0, 1, "iph")
-    iota(T.iy[:], [[2, 2]], 0, 16, "iy")
+    fill(T.c64[:], 64.0, "c64")
+    fill(uu[:, :, 0, :], 0.0, "u0")
+    fill(T.et[:], 0.0, "et")
     op("g", lambda: g.affine_select(T.i64[:], T.c64[:], [[-1, 128]], A.is_equal, 0.0, 0, 1), "c64", "i64")
-    iota(T.c8[:], [[0, 8], [64, 2]], -19, 0, "c8i", True)
-    iota(T.et[:], [[0, 2048]], 0, 0, "et", True)
-    for e in range(4):
-        iota(T.key[:, 32 * e:32 * e + 16], [[0, 8], [512, 2]], -31 - 32 * e, 0, "key%d" % e, True)
-        iota(T.key[:, 32 * e + 16:32 * e + 32], [[0, 8], [-512, 2]], 33 + 32 * e, 0, "key%d" % (e + 4), True)
-
-    fill(T.cst[:, 0:8], 2.0 ** -5, "cst0")
-    fill(T.cst[:, 8:16], 32.0, "cst1")
-    fill(T.cst[:, 16:24], 0.0, "cst2")
-    vs(k0[:, 0:1], T.ip[:, 0:1], 3, None, A.bitwise_and, "ip", "k0a")
-    scan(T.geo[:, 0:8], T.cst[:, 0:8], 64.0, "cst0 cst2", "geo0")
-    scan(T.geo[:, 8:16], T.cst[:, 8:16], 2.0 ** -9, "cst1 cst2", "geo1")
-    vc(kf[:, 0:1], k0[:, 0:1], "k0a", "kfa")
-    vs(k0[:, 8:16], T.ip[:], 14, None, A.bitwise_and, "ip", "k0b")
-    for y in range(2):
-        vc(T.ss[:, y:16:2], T.geo[:, 0:8], "geo0", "ss%d" % y)
-    vs(k0[:, 24:32], T.iph[:], 1, None, A.bitwise_and, "iph", "k0c")
-    vs(kf[:, 8:16], k0[:, 8:16], 8.0, None, A.mult, "k0b", "kfb")
-    vs(T.ai[0:32, :], T.ai0[0:32, :], kf[0:32, 0:1], 65536.0, A.add, "ai0 kfa", "aix", A.mult)
-    vc(T.ss[:, 16:32], T.ss[:, 0:16], "ss0 ss1", "ss2")
-    vt(kf[:, 16:24], kf[:, 8:16], k0[:, 24:32], A.add, "kfb k0c", "kfc")
-    vs(T.ai[0:32, :], T.ai[0:32, :], 7 * 4369.0, None, A.add, "aix", "ai")
-    vc(T.ss[:, 32:64], T.ss[:, 0:32], "ss0 ss1 ss2", "ss3")
-    vc(T.ul[:], kf[:, 16:24], "kfc", "ul")
-
-    vs(T.e8[0:32, :], T.nx4[0:32, 384:512], 8.0, None, A.mult, "nx4", "e8")
-    for e in range(4):
-        a = slice(128 * e, 128 * e + 128)
-        if e < 3:
-            vs(T.ep[0:32, a], T.nx4[0:32, a], 9 - 4 * e, 7 << (4 * e), A.logical_shift_right, "nx4", "ep%d" % e, A.bitwise_and)
-        else:
-            vs(T.ep[0:32, a], T.e8[0:32, :], 7 << 12, None, A.bitwise_and, "e8", "ep3")
-    vt(T.ep2[0:32, :], T.ep[0:32, 0:256], T.ep[0:32, 256:512], A.add, "ep0 ep1 ep2 ep3", "epx")
-    vt(T.pp[0:32, :], T.ep2[0:32, 0:128], T.ep2[0:32, 128:256], A.add, "epx", "pp")
-    vt(T.p4[0:32, :], T.pp[0:32, :], T.ai[0:32, :], A.add, "pp ai", "p4")
-    lst = []
-    for H in range(8):
-        for b in range(2):
-            z = (b + H) % 2
-            lst.append(("sy"[b], T.pr[16 * H + z:16 * H + 16:2, :], T.p4[0:32, 64 * b:64 * b + 64]))
-    dmas("dpr", lst, "p4", "pr")
-    vs(T.n4i[0:32, :], T.nx4[0:32, :], 511, None, A.bitwise_and, "nx4", "n4i")
-    vc(T.n4[0:32, :], T.n4i[0:32, :], "n4i", "n4")
-    dmas("dnr", [("sy"[z], T.nr[16 * H + z:16 * H + 16:2, :], T.n4[0:32, :]) for H in range(8) for z in range(2)], "n4", "nr")
+    for q in range(4):
+        iota(uu[quad(q), :, 0, 13], [[128, 2], [0, 2], [1, 4]], 0, 4, "ua%d" % q, "u0")
+    op("g", lambda: g.iota(T.i16[:], [[16, 8]], 0, 0), "", "i16")
+    iota(T.jj[:, 0:168], [[0, 8], [1, L]], 0, 0, "jj")
+    iota(T.idt[:], [[1, 256]], 0, 0, "idt")
+    UA = "u0 ua0 ua1 ua2 ua3 "
     for b in range(4):
         ac(T.et[:, 512 * b + b:512 * b + 512:4], T.i64[:], "i64 et", "et_%d" % b)
+    op("s", lambda: S.activation(uu[:, :, 0, 12], uu[:, :, 0, 13], AF.Identity, bias=-128.0), UA, "u12")
+
+    fill(cs[:, 0:4, :], 0.0, "cs0")
+    turn(T.nt[:], T.nxi[:], "nxi", "nt")
+    fill(cs[:, 4:6, :], 1.0, "cs1")
+    vc(uu[:, :, 1:5, 13], T.nt[:, 0:64], "nt", "y0")
+    vt(uu[:, :, 1:5, 5], T.nt[:, 64:128], T.nt[:, 0:64], A.subtract, "nt", "y1")
+    between = [lambda: fill(cs[:, 6:8, :], 2.0 ** -9, "cs2"),
+               lambda: (fill(cs[:, 0:2, 8:16], -1e29, "cs0"), fill(cs[:, 4, 4:8], 2.0, "cs1")),
+               lambda: (fill(cs[:, 2:4, 4:8], 1.0, "cs0"), fill(cs[:, 6:8, 0:16:8], 2.0 ** -9 / 24, "cs2")),
+               lambda: (fill(cs[:, 6:8, 1:16:8], 2.0 ** -9 / 6, "cs2 cs3"), fill(T.t1[:], 0.0, "t1"))]
+    for k in range(1, 5):
+        between[k - 1]()
+        src = slice(5 - k if k > 1 else 5, 16, 8)
+        vt(uu[:, :, 0:5 - k, 4 - k:16:8], uu[:, :, 1:6 - k, src], uu[:, :, 0:5 - k, src], A.subtract,
+           UA + "y0 y1" if k == 1 else "lv%d" % (k - 1), "lv%d" % k)
+    fill(cs[:, 6:8, 2:16:8], 2.0 ** -9 / 2, "cs3 cs4")
+    quant(T.qu[:], T.qus[:], T.ut[:], "ut", "qu")
+    turn(T.ct[:], cs[:], "cs0 cs1 cs2 cs3 cs4", "ct")
+    for m in range(4):
+        turn(T.tab[:, m:256:4], uu[:, m:16:4, 0, :], UA + "u12 lv1 lv2 lv3 lv4", "tab%d" % m)
+        if m == 0:
+            vc(T.g0[:], T.ali[:], "ali", "g0")
+        if m == 1:
+            vs(T.ul[:], T.i16[:], bit, None, A.add, "i16 ct", "ul")
 
     def score_mm(t, h):
-        a = slice(128 * h, 128 * h + 128)
-        mm(BANK[h], 128, T.qy[:], T.qys[:], T["qx%d" % t][:, a], T["qxs%d" % t][:, a], "qy qys qx%d" % t + "LH"[h])
+        mm(BANK[4 * h], 128, T.qy[:], T.qys[:], T["qx%d" % t][:, half(h)], T["qxs%d" % t][:, half(h)], "qy qys qx%d" % t + "LH"[h])
 
     def score_bits(h):
-        vs(T.sb[:, 128 * h:128 * h + 128], T[BANK[h]][:, 0:128], 0.0, 0.5, A.is_gt, BANK[h], "sb%d" % h, A.subtract)
+        vs(T.sb[:, half(h)], T[BANK[4 * h]][:, 0:128], thr, mul, A.is_gt, "ct " + BANK[4 * h], "sb%d" % h, A.mult)
+
+    def edge_turn(h):
+        turn(T.eg[0:32, half(h)], T.sb[0:32, half(h)], "sb%d" % h, "eg%d" % h)
+
+    def edge_add(h):
+        a = 128 * h
+        vt(T.ini[0:32, 84 * h + 11:84 * h + 84:L], T.eg[0:32, a + 4:a + 128:32], T.eg[0:32, a + 20:a + 128:32], A.add, "ini eg%d" % h, "in%d" % h)
+
+    def edge_scan(h):
+        scan(oo[0:32, h, 0:84], T.ini[0:32, 84 * h + 5:84 * h + 89], T.ini[0:32, 84 * h:84 * h + 84], "ini in%d" % h, "o00%d" % h)
 
     def send_state(t):
         k = "qx%dL qx%dH" % (t, t)
         send(T["qn%d" % t][:].bitcast(dt.uint8), T["qx%d" % t][:].bitcast(dt.uint8), "c", t, k, "qnc%d" % t)
         send(T["qns%d" % t][:], T["qxs%d" % t][:], "s", t, k, "qns%d" % t)
 
-    quant(T.qu[:], T.qus[:], T.ut[:], "ut", "qu")
-    turn(T.slt[:], T.sl[:], "sl", "slt")
+    def prefetch(h, lst, k):
+        ac(T.pg[:, half(h)], T.tab[:].indirect(lst), "ct tab0 tab1 tab2 tab3 " + k, "pg%d" % h, scl)
+
     vc(T.qy[:].bitcast(dt.uint32), T.qu[:].bitcast(dt.uint32).indirect(T.ul[:]), "qu ul", "qy")
     ac(T.qys[:], T.qus[:].indirect(T.ul[:]), "qu ul", "qys")
+    lists = [(T.g0[:, 0:8], "g0"), (T.g0[:, 8:16], "g0")]
+    prefetch(1, *lists[1])
+    prefetch(0, *lists[0])
     quant(T.qx0[:, 0:128], T.qxs0[:, 0:128], T.xl0[:], "xl0", "qx0L")
     quant(T.qx0[:, 128:256], T.qxs0[:, 128:256], T.xh0[:], "xh0", "qx0H")
-    iota(T.nw[:, 2048:2304], [[1, 256]], 0, 0, "nwi", True)
     send_state(0)
     score_mm(0, 0)
     score_mm(0, 1)
-    vs(k0[:, 32:34], T.ip[:, 0:2], 4, None, A.logical_shift_right, "ip", "k0e")
-    vc(T.lb[:, 0:16:2], T.slt[:, 0:256:34], "slt", "lb0")
-    vc(T.lb[:, 1:16:2], T.slt[:, 16:256:34], "slt", "lb1")
-    vs(k0[:, 16:17], k0[:, 32:33], 1, None, A.bitwise_and, "k0e", "k0d")
-    vs(kf[:, 32:34], k0[:, 32:34], -254.0, None, A.mult, "k0e", "kfe")
-    vs(T.c8[:], T.c8[:], 0.5, None, A.mult, "c8i", "c8")
-    vc(kf[:, 40:41], k0[:, 16:17], "k0d", "kfd")
-    vt(kf[:, 34:36], kf[:, 32:34], T.iy[:], A.add, "kfe iy", "kff")
-    vc(T.ss[:, 64:128], T.ss[:, 0:64], "ss0 ss1 ss2 ss3", "ss4")
-    vs(T.lb[:, 16:18], kf[:, 34:36], kf[:, 40:41], None, A.subtract, "kff kfd", "lbj")
+    vs(T.ini[:, 0:167], T.jj[:, 1:168], 13.0, None, A.is_ge, "jj", "ini")
+    fill(T.ini[:, 167:176], 0.0, "inp")
+    fill(oo[:, :, 84:105], 0.0, "oop")
+    ac(d1[:, 0:336:2], T.ini[:, 0:168], "ini inp", "d1a")
+    ac(d1[:, L:L + 336:2], T.ini[:, 0:168], "ini inp", "d1b")
     score_bits(0)
-    score_bits(1)
-    vc(T.norm[:, 0:16:2], T.geo[:, 8:16], "geo1", "norm0")
-    vs(T.norm[:, 1:16:2], T.geo[:, 8:16], -1.0, None, A.mult, "geo1", "norm1")
-    for r in range(4):
-        (ac if r % 2 else vc)(T.pw[:, r:256:4], T.pr[:, 64 * r:64 * r + 64], "pr", "pw%d" % r)
+    fill(T.ini[:, 10:168:L], -2.0, "ini inp")
+    edge_turn(0)
+    quant(T.qe[:, 0:128], T.qes[:, 0:128], T.et[:, 0:512], "et et_0", "qe0")
+    edge_add(0)
+    fill(d1[:, 20:20 + 16 * L:L], BIG, "d1a d1b")
+    edge_scan(0)
+    fill(d1[:, 22:22 + 16 * L:L], -BIG - 3.0, "d1a d1b d1c")
 
-    def prefetch_pick():
-        ac(T.pg[:], T.pw[:].indirect(T.lb[:, 0:16]), "pw0 pw1 pw2 pw3 lb0 lb1", "pg")
-
-    def prefetch_1():
-        turn(T.pt[:], T.pg[:], "pg", "pt")
-        vc(T.pc[:, 0:16], T.pt[:, 0:256:17], "pt", "pc0")
-        vc(T.pc[:, 16:32:2], T.pt[:, 1:256:34], "pt", "pc1")
-        vc(T.pc[:, 17:32:2], T.pt[:, 16:256:34], "pt", "pc2")
-
-    def prefetch_2():
-        vs(T.am[:], T.pc[:, 0:16], 16, None, A.logical_shift_right, "pc0", "am")
-        for e in range(4):
-            vs(T.ei[:, 32 * e:32 * e + 32], T.pc[:], 4 * e, 7, A.logical_shift_right, "pc0 pc1 pc2", "ei%d" % e, A.bitwise_and)
-        vs(T.yi[:], T.am[:], 2.0 ** -8, 8.0, A.mult, "am", "yi", A.add)
-        vt(T.ek[:], T.ei[:], T.key[:], A.add, "ei0 ei1 ei2 ei3 " + " ".join("key%d" % k for k in range(8)), "ek")
-        vt(T.amc[:], T.yi[:], T.c8[:], A.add, "yi c8", "amc")
-        vt(T.dd[:], T.ek[:], T.ss[:], A.mult, "ek ss0 ss1 ss2 ss3 ss4", "dd")
-
-    def bits_pick():
-        ac(T.bg[:, 160:288], T.sb[:].indirect(T.lb[:, 10:18]), "sb0 sb1 lb0 lb1 lbj", "bg1")
-        vc(T.bg[:, 0:160], T.sb[:].indirect(T.lb[:, 0:10]), "sb0 sb1 lb0 lb1", "bg0")
-
-    prefetch_pick()
-    bits_pick()
-    quant(T.qe[:], T.qes[:], T.et[:], "et et_0 et_1 et_2 et_3", "qe")
-    for r in range(4):
-        ac(T.nw[:, r:2048:4], T.nr[:, 512 * r:512 * r + 512], "nr", "nw%d" % r)
-    NW = "nw0 nw1 nw2 nw3 nwi "
-    prefetch_1()
-    prefetch_2()
-
-    bt, val, tmp = T.bt, T.val, T.tmp
     for t in range(R):
         ts = "%d" % t
-        gl, ga = T["gl" + ts], T["ga" + ts]
-        halves = (("f", T.f, [2, 3, 4, 5], "qx", "qx%dL qx%dH" % (t, t)), ("fa", T.fa, [6, 7, 0, 1], "qn", "qnc%d qns%d" % (t, t)))
-        if t:
-            bits_pick()
-        for _, _, bk, q, k in halves:
+        gl, go, ga = T["gl" + ts], T["go" + ts], T["ga" + ts]
+        score_bits(1)
+        if t == 0:
+            for b in range(1, 4):
+                quant(T.qe[:, half(b)], T.qes[:, half(b)], T.et[:, 512 * b:512 * b + 512], "et et_%d" % b, "qe%d" % b)
+        for n, bk, q, k in (("f", [1, 2, 3, 5], "qx", "qx%dL qx%dH" % (t, t)), ("fa", [6, 7, 0, 4], "qn", "qnc%d qns%d" % (t, t))):
             for b in range(4):
-                a = slice(128 * b, 128 * b + 128)
-                mm(BANK[bk[b]], 256, T.qe[:, a], T.qes[:, a], T[q + ts][:], T[q + "s" + ts][:], "qe " + k)
-        turn(bt[:, 256:288], T.bg[:, 256:288], "bg1", "bte")
-        vs(wk[:, 0:1], bt[:, 257:258], 64.0, 80.0, A.mult, "bte", "w0", A.add)
-        op("s", lambda: S.activation(wk[:, 8:9], bt[:, 272:273], AF.Identity, bias=432.0, scale=-64.0), "bte", "w1")
-        turn(bt[:, 0:256], T.bg[:, 0:256], "bg0 bg1", "bt")
-        vs(val[:, 0:1], bt[:, 259:260], 32.0, wk[:, 0:1], A.mult, "bte w0", "val0", A.add)
-        op("s", lambda: S.activation(val[:, 1:2], bt[:, 274:275], AF.Identity, bias=wk[:, 8:9], scale=-32.0), "bte w1", "val1")
-        x0, x1, x2, o = wk[:, 32:46], wk[:, 48:62], wk[:, 64:78], T.ou
+                mm(BANK[bk[b]], 256, T.qe[:, half(b)], T.qes[:, half(b)], T[q + ts][:], T[q + "s" + ts][:], "qe%d " % b + k)
+                ac(T[n][:, 256 * b:256 * b + 256], T[BANK[bk[b]]][:, 0:256], BANK[bk[b]], "%s_%d" % (n, b), 0.015625)
 
-        def last(y):
-            i = 14 + y
-            vs(wk[:, 46 + y:47 + y], val[:, i:i + 1], (-1.0) ** y * 2.0 ** 31, wk[:, 16 + i:17 + i], A.mult, "val%d b3" % i, "l%d" % y, A.add)
+        def pick(h):
+            vt(T.gm[:, half(h)], T.sb[:].indirect(lists[h][0]), T.pg[:, half(h)], A.mult, "sb0 sb1 pg%d %s" % (h, lists[h][1]), "gm%d" % h)
 
-        def last2(y):
-            i = 14 + y
-            vs(o[:, i:i + 1], wk[:, 46 + y:47 + y], T.yi[:, i:i + 1], 256.0, A.min, "l%d yi" % y, "ou%d" % y, A.mult)
-
-        for i in range(14):
-            c, d = slice(8 * i, 8 * i + 8), T.dd[:, i:128:16]
-            me, sg, new = val[:, i:i + 1], bt[:, 17 * i:17 * i + 1], val[:, i + 2:i + 3]
-            if i % 2:
-                op("s", lambda: S.activation(tmp[:, c], d, AF.Abs, bias=me, scale=sg), "dd bt val%d" % i, "tmp%d" % i)
-                op("s", lambda: S.activation(T.jk[:, c], tmp[:, c], AF.Relu, bias=16.0 * 32.0 ** -(i // 2), scale=-1.0, accum_out=new),
-                   "tmp%d" % i, "jk%d val%d" % (i, i + 2))
-            else:
-                vs(tmp[:, c], d, sg, me, A.mult, "dd bt val%d" % i, "tmp%d" % i, A.subtract)
-                if i == 2:
-                    vt(wk[:, 16:32], bt[:, 0:256:17], T.amc[:], A.add, "bt amc", "b3")
-                op("v", lambda: V.tensor_reduce(new, tmp[:, c], AxisListType.X, A.min, apply_absolute_value=True), "tmp%d" % i, "val%d" % (i + 2))
-        vt(x0, val[:, 0:14], T.norm[:, 0:14], A.mult, "norm0 norm1 " + " ".join("val%d" % i for i in range(14)), "t1")
-        last(0)
-        vt(x1, x0, wk[:, 16:30], A.add, "t1 b3", "t2")
-        last2(0)
-        vt(x2, x1, T.yi[:, 0:14], A.min, "t2 yi", "t3")
-        last(1)
-        vs(o[:, 0:14], x2, 256.0, None, A.mult, "t3", "ou")
-        last2(1)
-        vc(T.nu[:], T.nw[:].indirect(o[:]), NW + "ou ou0 ou1", "nu")
-        if t < R - 1:
-            ac(T.nbf[:], T.nw[:].indirect(o[:]), NW + "ou ou0 ou1", "nbf")
-        dmas("dgl" + ts, [("ys"[k % 2], gl[16 * k:16 * k + 16, :], T.nu[2 * k:128:16, 32 * k:32 * k + 32]) for k in range(8)], "nu", "gl" + ts)
-        if t < R - 1:
-            co = T["co" + ts]
-            turn(T.at[:], T.nbf[:], "nbf", "at")
-            vc(co[:], T.at[:, 0:256:17], "at", "co" + ts)
-            send(T["ca" + ts][:], co[:], "l", t, "co" + ts, "ca" + ts)
-        send(ga[:], gl[:, 8:16], "g", t, "gl" + ts, "ga" + ts)
-        for n, f, bk, _, _ in halves:
-            for b in range(4):
-                bank = BANK[bk[b]]
-                fo, fi = f[:, 256 * b:256 * b + 256], T[bank][:, 0:256]
-                if b % 2:
-                    vs(fo, fi, 0.015625, None, A.mult, bank, "%s_%d" % (n, b))
+        pick(1)
+        edge_turn(1)
+        pick(0)
+        edge_add(1)
+        turn(T.tb[:, half(1)], T.gm[:, half(1)], "gm1", "tb1")
+        edge_scan(1)
+        turn(T.tb[:, half(0)], T.gm[:, half(0)], "gm0", "tb0")
+        for k in range(5):
+            vt(d1[:, 10 + 2 * k:10 + 2 * k + 16 * L:L], T.tb[:, k:256:16], T.tb[:, 8 + k:256:16], A.add, "d1a d1b d1c tb0 tb1", "d%d" % k)
+        D = "oop d1a d1b d1c d0 d1 d2 d3 d4 "
+        for gr in range(8):
+            q, x = gr // 2, gr % 2
+            for h in (1, 0):
+                a = 168 * h + L * x
+                if gr == 7:
+                    scan(oo[:, 4 + h, 0:84], oo[:, 2 + h, 5:89], d1[:, a:a + 168:2], D + " ".join("o%d1%d" % (k, h) for k in range(4)), "of%d" % h)
                 else:
-                    ac(fo, fi, bank, "%s_%d" % (n, b), 0.015625)
-            if n == "f" and t < R - 1:
-                if t == 0:
-                    vs(k0[:, 40:41], T.ip[:, 0:1], 8, None, A.bitwise_and, "ip", "k0m")
-                    vs(kf[:, 56:57], k0[:, 40:41], 0.0, None, A.is_equal, "k0m", "mlo")
-                    vs(kf[:, 57:58], k0[:, 40:41], 0.0, None, A.is_gt, "k0m", "mhi")
-                vs(wk[:, 80:96], co[:], kf[:, 56:57], None, A.mult, "mlo co" + ts, "m1")
+                    scan(oo[quad(q + x), 2 * (1 - x) + h, 0:84], oo[quad(q), 2 * x + h, 5:89], d1[quad(q), a:a + 168:2],
+                         D + "o%d%d%d" % (q, x, h), "o%d%d%d" % (q + x, 1 - x, h))
+        vt(T.t1[:, :, 0:4], oo[:, 2:6, 9:84:L], oo[:, 2:6, 14:84:L], A.subtract,
+           "of0 of1 " + " ".join("o%d1%d" % (k, h) for k in range(4) for h in range(2)), "t1")
+        turn(T.t2[:], T.t1[:], "t1", "t2")
+        for c in range(2):
+            turn(T.t3[:, c:64:2], T.t2[:, :, c, :], "t2", "t3%d" % c)
+        vs(go[:], T.t3[:, 32:40], 512.0, 128.25, A.mult, "t30 t31", "go" + ts, A.add)
+        vs(gl[:], T.t3[:, 0:8], 512.0, 128.25, A.mult, "t30 t31", "gl" + ts, A.add)
+        send(ga[:], go[:], "g", t, "go" + ts, "ga" + ts)
+        lists = [(gl[:], "gl" + ts), (ga[:], "ga" + ts)]
 
         def make_z(h):
-            k, n, off, ok = "lh"[h] + ts, ("f", "fa")[h], (gl[:, 0:8], ga[:])[h], ("gl", "ga")[h] + ts
+            k, n = "lh"[h] + ts, ("f", "fa")[h]
             z = T["z" + k]
             for b in range(4):
-                (vc if b < 2 else ac)(z[:, b:512:4], T[n][:, 256 * b:256 * b + 256].indirect(off), "%s_%d %s" % (n, b, ok), "z%s_%d" % (k, b))
+                (vc if b < 2 else ac)(z[:, b:512:4], T[n][:, 256 * b:256 * b + 256].indirect(lists[h][0]), "%s_%d %s" % (n, b, lists[h][1]), "z%s_%d" % (k, b))
             quant(T["q" + k][:], T["q" + "lh"[h] + "s" + ts][:], z[:], " ".join("z%s_%d" % (k, b) for b in range(4)), "q" + k)
 
         def make_r(h):
             q, qs, kk = T["q" + "lh"[h] + ts], T["q" + "lh"[h] + "s" + ts], "q" + "lh"[h] + ts
             for b in range(4):
-                a = slice(128 * b, 128 * b + 128)
-                mm(BANK[4 * h + b], 128, T.lw[:, a], T.lws[:, a], q[:], qs[:], "lw " + kk, True, False)
-                mm(BANK[4 * h + b], 128, T.qe[:, a], T.qes[:, a], q[:], qs[:], "qe " + kk, False, True)
+                mm(BANK[4 * h + b], 128, T.lw[:, half(b)], T.lws[:, half(b)], q[:], qs[:], "lw " + kk, True, False)
+                mm(BANK[4 * h + b], 128, T.qe[:, half(b)], T.qes[:, half(b)], q[:], qs[:], "qe%d " % b + kk, False, True)
 
         def make_x(h):
-            a, xk = slice(128 * h, 128 * h + 128), "x%s%d" % ("lh"[h], t + 1)
+            a, xk = half(h), "x%s%d" % ("lh"[h], t + 1)
             for b in range(4):
                 bank = BANK[4 * h + b]
                 xo, xi, w = T[xk][:, b:512:4], T[bank][:, 0:128], "%s_%d" % (xk, b)
@@ -365,39 +306,40 @@ def rank_program(g, core, T, topo):
             qn, qns, key = T["qx%d" % (t + 1)], T["qxs%d" % (t + 1)], "qx%d%s" % (t + 1, "LH"[h])
             quant(qn[:, a], qns[:, a], T[xk][:], " ".join("%s_%d" % (xk, b) for b in range(4)), key)
             if t < R - 1:
-                score_mm(t + 1, h)
                 return
-            mm(BANK[h], 128, T.qv[:], T.qvs[:], qn[:, a], qns[:, a], "qv " + key)
+            mm(BANK[4 * h], 128, T.qv[:], T.qvs[:], qn[:, a], qns[:, a], "qv " + key)
             lst = [("y", T.oc[:, 512 * h:512 * h + 512], qn[:, a].bitcast(dt.uint8))]
             lst += [("y", T.osc[4 * k:4 * k + 4, a], qns[32 * k:32 * k + 4, a]) for k in range(4)]
             dmas("doc" + "lh"[h], lst, key, "")
-            ac(T.oaf[:, a], T.nw[:, 2048:2304].indirect(ga[:] if h else gl[:, 0:8]), "nwi " + ("ga" if h else "gl") + ts, "oa%d" % h)
-            ac(T.ys[:, a], T[BANK[h]][:, 0:128], BANK[h], "ys%d" % h)
+            ac(T.ys[:, a], T[BANK[4 * h]][:, 0:128], BANK[4 * h], "ys%d" % h)
             dmas("dy" + "lh"[h], [("s", T.y[:, a], T.ys[:, a])], "ys%d" % h, "")
 
+        def addresses(h):
+            ac(T.oaf[:, half(h)], T.idt[:].indirect(lists[h][0]), "idt " + lists[h][1], "oa%d" % h)
+
+        after = prefetch if t < R - 1 else lambda h, a, b: addresses(h)
         make_z(0)
         make_r(0)
-        if t < R - 1:
-            vs(wk[:, 96:112], T["ca" + ts][:], kf[:, 57:58], None, A.mult, "mhi ca" + ts, "m2")
-            vt(wk[:, 32:48], wk[:, 80:96], wk[:, 96:112], A.add, "m1 m2", "t1 l0 l1")
-            vc(T.lb[:, 0:16], wk[:, 32:48], "t1", "lb0 lb1")
-            prefetch_pick()
-            make_x(0)
-            prefetch_1()
-            make_z(1)
-            make_r(1)
-            score_bits(0)
-            prefetch_2()
-            make_x(1)
-            send_state(t + 1)
-            score_bits(1)
-        else:
+        after(0, *lists[0])
+        if t == R - 1:
             quant(T.qv[:], T.qvs[:], T.vt[:], "vt", "qv")
-            make_x(0)
-            make_z(1)
-            make_r(1)
-            make_x(1)
-    dmas("doa", [("y", T.oa[:], T.oaf[0:128:16, :])], "oa0 oa1", "")
+        make_x(0)
+        make_z(1)
+        if t < R - 1:
+            score_mm(t + 1, 0)
+        make_r(1)
+        after(1, *lists[1])
+        if t < R - 1:
+            score_bits(0)
+            edge_turn(0)
+            edge_add(0)
+            edge_scan(0)
+        else:
+            dmas("doa", [("y", T.oa[:], T.oaf[0:128:16, :])], "oa0 oa1", "")
+        make_x(1)
+        if t < R - 1:
+            send_state(t + 1)
+            score_mm(t + 1, 1)
     for s in sorted(cnt):
         if known["g"].get(s, 0) < cnt[s]:
             g.wait_ge(T.sem[s], cnt[s])

@@ -9,8 +9,8 @@ SCRATCH = {}
 for _d, _l in (
         ("int32", "nxi:128 nt:128 ali:16 i16:8"),
         ("float32", "uu:16,5,16 tab:256 cs:8,16 ct:8,16 jj:176 d1:360 ini:176 oo:6,105 pg:256 gm:256 tb:256 "
-                    "t1:4,16 t2:2,2,16 t3:64 idt:256 oaf:256 ys:256"),
-        ("bfloat16", "i64:128 c64:128 et:2048 ut:512 vt:512 sb:256 eg:256 f:1024 fa:1024 "
+                    "t1:2,2,32 t2l:2,2,16 t2h:2,2,16 t3:2,64 idt:256 oaf:256 ys:256"),
+        ("bfloat16", "i64:128 c64:128 et:2048 ut:512 vt:512 sb:256 eg:256 fl:1024 fh:1024 "
                      "xl0:512 xl1:512 xl2:512 xl3:512 xh0:512 xh1:512 xh2:512 xh3:512 "
                      "zl0:512 zl1:512 zl2:512 zh0:512 zh1:512 zh2:512"),
         ("uint16", "ul:8 g0:16 gl0:8 gl1:8 gl2:8 go0:8 go1:8 go2:8 ga0:8 ga1:8 ga2:8")):
@@ -26,6 +26,14 @@ for _s in BANK:
     SCRATCH[_s] = ("psum", [128, 512], "float32")
 SEMAPHORES = ("cv cs ct cg dnx dal dxl dxh du dv dw dyl dyh doa docl doch".split()
               + [n + "%d" % t for n in ("rc", "lc", "rs", "ls", "rg", "lg") for t in range(R)])
+FIRST = "bL eL bH aL iL"
+NEXT = "bH iL"
+CARRY = ("pH eH fL0 fL1 fL2 tH DH aH dH0 dH1 iH dH2 dH3 fL3 pL sH0 tL DL sH1 dL0 dL1 sH2 dL2 dL3 fH0 fH1 fH2 fH3 "
+         "sH3 sL0 sH4 sL1 sH5 sL2 sH6 sL3 sH7 sL4 nH sL5 uH sL6 vH sL7 wH nL uL vL wL")
+STATE = ("zL0 zL1 zL2 zL3 qL rL0 rL1 rL2 rL3 gL zH0 zH1 zH2 zH3 qH rH0 rH1 rH2 rH3 XL0 xL1 XL2 xL3 QL mL "
+         "XH0 xH1 XH2 xH3 gH bL QH mH eL aL")
+LAST = ("zL0 zL1 zL2 zL3 qL rL0 rL1 rL2 rL3 VL gL zH0 zH1 zH2 zH3 qH rH0 rH1 rH2 rH3 XL0 xL1 XL2 xL3 QL mL "
+        "XH0 xH1 XH2 xH3 QH mH gH OL yL yH")
 
 
 def rank_program(g, core, T, topo):
@@ -120,6 +128,9 @@ def rank_program(g, core, T, topo):
     def fill(ap, c, w):
         op("v", lambda: V.memset(ap, c), "", w)
 
+    def const(ap, n, c, w):
+        ac(ap, T.c64[:, 0:n], "c64", w, c / 64.0)
+
     def quant(o, s, i, r, w):
         op("v", lambda: V.quantize_mx(o, s, i), r, w)
 
@@ -144,202 +155,179 @@ def rank_program(g, core, T, topo):
     uu, cs, d1, oo = T.uu, T.cs, T.d1, T.oo
     thr, bit, mul, scl = [T.ct[:, 2 * k, 0:1] for k in range(4)]
     dmas("dnx", [("y", T.nxi[:], T.nx[:])], "", "nxi")
-    dmas("du", [("s", T.ut[:], T.u[:])], "", "ut")
-    dmas("dxl", [("y", T.xl0[:], T.x[:, 0:512])], "", "xl0")
+    dmas("dal", [("s", T.ali[:], T.al[:])], "", "ali")
+    dmas("du", [("y", T.ut[:], T.u[:])], "", "ut")
     dmas("dxh", [("s", T.xh0[:], T.x[:, 512:1024])], "", "xh0")
-    dmas("dal", [("y", T.ali[:], T.al[:])], "", "ali")
-    dmas("dw", [("y", T.lw[:].bitcast(dt.uint8), T.wc[:]), ("y", T.lws[:], T.ws[:])], "", "lw")
+    dmas("dxl", [("y", T.xl0[:], T.x[:, 0:512])], "", "xl0")
+    dmas("dw", [("y", T.lw[:].bitcast(dt.uint8), T.wc[:]), ("y", T.lws[:], T.ws[:])], "xl0 xh0", "lw")
     dmas("dv", [("y", T.vt[:], T.v[:])], "", "vt")
 
     fill(T.c64[:], 64.0, "c64")
-    fill(uu[:, :, 0, :], 0.0, "u0")
     fill(T.et[:], 0.0, "et")
-    op("g", lambda: g.affine_select(T.i64[:], T.c64[:], [[-1, 128]], A.is_equal, 0.0, 0, 1), "c64", "i64")
-    for q in range(4):
-        iota(uu[quad(q), :, 0, 13], [[128, 2], [0, 2], [1, 4]], 0, 4, "ua%d" % q, "u0")
-    op("g", lambda: g.iota(T.i16[:], [[16, 8]], 0, 0), "", "i16")
     iota(T.jj[:, 0:168], [[0, 8], [1, L]], 0, 0, "jj")
+    op("g", lambda: g.affine_select(T.i64[:], T.c64[:], [[-1, 128]], A.is_equal, 0.0, 0, 1), "c64", "i64")
+    op("g", lambda: g.iota(T.i16[:], [[16, 8]], 0, 0), "", "i16")
+    for q in range(4):
+        iota(uu[quad(q), :, 0, 13], [[128, 2], [0, 2], [1, 4]], 0, 4, "ua%d" % q)
     iota(T.idt[:], [[1, 256]], 0, 0, "idt")
-    UA = "u0 ua0 ua1 ua2 ua3 "
+    slots = [(0, 4, 0, 4, 1, 0.0), (0, 2, 4, 8, 1, 0.0), (0, 2, 8, 16, 1, -1e29), (2, 6, 8, 16, 1, 1.0), (2, 4, 4, 8, 1, 1.0),
+             (4, 6, 0, 4, 1, 1.0), (4, 5, 4, 8, 1, 2.0), (5, 6, 4, 8, 1, 1.0), (6, 8, 4, 8, 1, 1.0), (6, 8, 11, 16, 1, 2.0 ** -9)]
+    slots += [(6, 8, k, 11 if k == 3 else 16, 8, 2.0 ** -9 / f) for k, f in enumerate((24, 6, 2, 1))]
+    for k, (a, b, c, d, e, val) in enumerate(slots):
+        const(cs[:, a:b, c:d:e], (b - a) * len(range(c, d, e)), val, "cs%d" % k)
     for b in range(4):
         ac(T.et[:, 512 * b + b:512 * b + 512:4], T.i64[:], "i64 et", "et_%d" % b)
+    turn(T.ct[:], cs[:], " ".join("cs%d" % k for k in range(len(slots))), "ct")
+    vs(T.ini[:, 0:167], T.jj[:, 1:168], 13.0, None, A.is_ge, "jj", "ini")
+    vs(T.ul[:], T.i16[:], bit, None, A.add, "i16 ct", "ul")
+    for b in range(4):
+        quant(T.qe[:, half(b)], T.qes[:, half(b)], T.et[:, 512 * b:512 * b + 512], "et et_%d" % b, "qe%d" % b)
+    const(uu[:, :, 0, 4:8], 64, 0.0, "u0")
+    const(uu[:, :, 0, 14:16], 32, 0.0, "u1")
+    const(T.ini[:, 167:176], 9, 0.0, "inp")
+    const(T.t1[:], 128, 0.0, "t10 t11")
+    const(oo[:, :, 84:105], 126, 0.0, "oop")
+    ac(d1[:, 0:336:2], T.ini[:, 0:168], "ini inp", "d1a")
+    ac(d1[:, L:L + 336:2], T.ini[:, 0:168], "ini inp", "d1b")
+    UA = "u0 u1 ua0 ua1 ua2 ua3 "
     op("s", lambda: S.activation(uu[:, :, 0, 12], uu[:, :, 0, 13], AF.Identity, bias=-128.0), UA, "u12")
-
-    fill(cs[:, 0:4, :], 0.0, "cs0")
-    turn(T.nt[:], T.nxi[:], "nxi", "nt")
-    fill(cs[:, 4:6, :], 1.0, "cs1")
-    vc(uu[:, :, 1:5, 13], T.nt[:, 0:64], "nt", "y0")
-    vt(uu[:, :, 1:5, 5], T.nt[:, 64:128], T.nt[:, 0:64], A.subtract, "nt", "y1")
-    between = [lambda: fill(cs[:, 6:8, :], 2.0 ** -9, "cs2"),
-               lambda: (fill(cs[:, 0:2, 8:16], -1e29, "cs0"), fill(cs[:, 4, 4:8], 2.0, "cs1")),
-               lambda: (fill(cs[:, 2:4, 4:8], 1.0, "cs0"), fill(cs[:, 6:8, 0:16:8], 2.0 ** -9 / 24, "cs2")),
-               lambda: (fill(cs[:, 6:8, 1:16:8], 2.0 ** -9 / 6, "cs2 cs3"), fill(T.t1[:], 0.0, "t1"))]
-    for k in range(1, 5):
-        between[k - 1]()
-        src = slice(5 - k if k > 1 else 5, 16, 8)
-        vt(uu[:, :, 0:5 - k, 4 - k:16:8], uu[:, :, 1:6 - k, src], uu[:, :, 0:5 - k, src], A.subtract,
-           UA + "y0 y1" if k == 1 else "lv%d" % (k - 1), "lv%d" % k)
-    fill(cs[:, 6:8, 2:16:8], 2.0 ** -9 / 2, "cs3 cs4")
-    quant(T.qu[:], T.qus[:], T.ut[:], "ut", "qu")
-    turn(T.ct[:], cs[:], "cs0 cs1 cs2 cs3 cs4", "ct")
-    for m in range(4):
-        turn(T.tab[:, m:256:4], uu[:, m:16:4, 0, :], UA + "u12 lv1 lv2 lv3 lv4", "tab%d" % m)
-        if m == 0:
-            vc(T.g0[:], T.ali[:], "ali", "g0")
-        if m == 1:
-            vs(T.ul[:], T.i16[:], bit, None, A.add, "i16 ct", "ul")
+    const(T.ini[:, 10:168:L], 8, -2.0, "ini inp")
+    const(d1[:, 20:20 + 16 * L:L], 16, BIG, "d1a d1b")
+    const(d1[:, 22:22 + 16 * L:L], 16, -BIG - 3.0, "d1a d1b d1c")
 
     def score_mm(t, h):
         mm(BANK[4 * h], 128, T.qy[:], T.qys[:], T["qx%d" % t][:, half(h)], T["qxs%d" % t][:, half(h)], "qy qys qx%d" % t + "LH"[h])
-
-    def score_bits(h):
-        vs(T.sb[:, half(h)], T[BANK[4 * h]][:, 0:128], thr, mul, A.is_gt, "ct " + BANK[4 * h], "sb%d" % h, A.mult)
-
-    def edge_turn(h):
-        turn(T.eg[0:32, half(h)], T.sb[0:32, half(h)], "sb%d" % h, "eg%d" % h)
-
-    def edge_add(h):
-        a = 128 * h
-        vt(T.ini[0:32, 84 * h + 11:84 * h + 84:L], T.eg[0:32, a + 4:a + 128:32], T.eg[0:32, a + 20:a + 128:32], A.add, "ini eg%d" % h, "in%d" % h)
-
-    def edge_scan(h):
-        scan(oo[0:32, h, 0:84], T.ini[0:32, 84 * h + 5:84 * h + 89], T.ini[0:32, 84 * h:84 * h + 84], "ini in%d" % h, "o00%d" % h)
 
     def send_state(t):
         k = "qx%dL qx%dH" % (t, t)
         send(T["qn%d" % t][:].bitcast(dt.uint8), T["qx%d" % t][:].bitcast(dt.uint8), "c", t, k, "qnc%d" % t)
         send(T["qns%d" % t][:], T["qxs%d" % t][:], "s", t, k, "qns%d" % t)
 
-    def prefetch(h, lst, k):
-        ac(T.pg[:, half(h)], T.tab[:].indirect(lst), "ct tab0 tab1 tab2 tab3 " + k, "pg%d" % h, scl)
+    def prefetch(h):
+        ac(T.pg[:, half(h)], T.tab[:].indirect(lists[h][0]), "ct tab0 tab1 tab2 tab3 " + lists[h][1], "pg%d" % h, scl)
 
+    def level(k):
+        src = slice(5 - k if k > 1 else 5, 16, 8)
+        vt(uu[:, :, 0:5 - k, 4 - k:16:8], uu[:, :, 1:6 - k, src], uu[:, :, 0:5 - k, src], A.subtract,
+           UA + "y0 y1" if k == 1 else "lv%d" % (k - 1), "lv%d" % k)
+
+    lists = [(T.g0[:, 0:8], "g0"), (T.g0[:, 8:16], "g0")]
+    turn(T.nt[:], T.nxi[:], "nxi", "nt")
+    vc(T.g0[:], T.ali[:], "ali", "g0")
+    vc(uu[:, :, 1:5, 13], T.nt[:, 0:64], "nt", "y0")
+    vt(uu[:, :, 1:5, 5], T.nt[:, 64:128], T.nt[:, 0:64], A.subtract, "nt", "y1")
+    quant(T.qu[:], T.qus[:], T.ut[:], "ut", "qu")
+    level(1)
     vc(T.qy[:].bitcast(dt.uint32), T.qu[:].bitcast(dt.uint32).indirect(T.ul[:]), "qu ul", "qy")
     ac(T.qys[:], T.qus[:].indirect(T.ul[:]), "qu ul", "qys")
-    lists = [(T.g0[:, 0:8], "g0"), (T.g0[:, 8:16], "g0")]
-    prefetch(1, *lists[1])
-    prefetch(0, *lists[0])
-    quant(T.qx0[:, 0:128], T.qxs0[:, 0:128], T.xl0[:], "xl0", "qx0L")
+    level(2)
     quant(T.qx0[:, 128:256], T.qxs0[:, 128:256], T.xh0[:], "xh0", "qx0H")
-    send_state(0)
+    level(3)
+    quant(T.qx0[:, 0:128], T.qxs0[:, 0:128], T.xl0[:], "xl0", "qx0L")
     score_mm(0, 0)
     score_mm(0, 1)
-    vs(T.ini[:, 0:167], T.jj[:, 1:168], 13.0, None, A.is_ge, "jj", "ini")
-    fill(T.ini[:, 167:176], 0.0, "inp")
-    fill(oo[:, :, 84:105], 0.0, "oop")
-    ac(d1[:, 0:336:2], T.ini[:, 0:168], "ini inp", "d1a")
-    ac(d1[:, L:L + 336:2], T.ini[:, 0:168], "ini inp", "d1b")
-    score_bits(0)
-    fill(T.ini[:, 10:168:L], -2.0, "ini inp")
-    edge_turn(0)
-    quant(T.qe[:, 0:128], T.qes[:, 0:128], T.et[:, 0:512], "et et_0", "qe0")
-    edge_add(0)
-    fill(d1[:, 20:20 + 16 * L:L], BIG, "d1a d1b")
-    edge_scan(0)
-    fill(d1[:, 22:22 + 16 * L:L], -BIG - 3.0, "d1a d1b d1c")
+    send_state(0)
+    level(4)
+    for m in range(4):
+        turn(T.tab[:, m:256:4], uu[:, m:16:4, 0, :], UA + "u12 lv1 lv2 lv3 lv4", "tab%d" % m)
+    prefetch(1)
+    prefetch(0)
+
+    def step(t, name):
+        c, h, k = name[0], "LH".index(name[1]), int(name[2:] or 0)
+        ts, H, lh = "%d" % t, "%d" % h, "lh"[h]
+        a, bank = 128 * h, BANK[4 * h + k % 4]
+        if c == "b":
+            vs(T.sb[:, half(h)], T[bank][:, 0:128], thr, mul, A.is_gt, "ct " + bank, "sb" + H, A.mult)
+        elif c == "e":
+            turn(T.eg[0:32, half(h)], T.sb[0:32, half(h)], "sb" + H, "eg" + H)
+        elif c == "a":
+            vt(T.ini[0:32, 84 * h + 11:84 * h + 84:L], T.eg[0:32, a + 4:a + 128:32], T.eg[0:32, a + 20:a + 128:32], A.add, "ini eg" + H, "in" + H)
+        elif c == "i":
+            scan(oo[0:32, h, 0:84], T.ini[0:32, 84 * h + 5:84 * h + 89], T.ini[0:32, 84 * h:84 * h + 84], "ini inp in" + H, "o00" + H)
+        elif c == "f":
+            bank, q = BANK[[[1, 2, 3, 5], [6, 7, 0, 4]][h][k]], ("qx", "qn")[h]
+            mm(bank, 256, T.qe[:, half(k)], T.qes[:, half(k)], T[q + ts][:], T[q + "s" + ts][:],
+               "qe%d " % k + ("qx%sL qx%sH", "qnc%s qns%s")[h] % (ts, ts))
+            ac(T["f" + lh][:, 256 * k:256 * k + 256], T[bank][:, 0:256], bank, "f%s%d" % (lh, k), 0.015625)
+        elif c == "p":
+            vt(T.gm[:, half(h)], T.sb[:].indirect(lists[h][0]), T.pg[:, half(h)], A.mult, "sb0 sb1 pg%d %s" % (h, lists[h][1]), "gm" + H)
+        elif c == "t":
+            turn(T.tb[:, half(h)], T.gm[:, half(h)], "gm" + H, "tb" + H)
+        elif c == "d":
+            vt(d1[:, 168 * h + 10 + 2 * k:168 * h + 168:L], T.tb[:, a + k:a + 128:16], T.tb[:, a + 8 + k:a + 128:16], A.add,
+               "d1a d1b d1c tb" + H, "d%d%d" % (h, k))
+        elif c == "D":
+            ac(d1[:, 168 * h + 18:168 * h + 168:L], T.tb[:, a + 12:a + 128:16], "d1a d1b d1c tb" + H, "d%d4" % h)
+        elif c == "s":
+            q, x = k // 2, k % 2
+            D, a = "oop d1a d1b d1c " + " ".join("d%d%d" % (h, j) for j in range(5)), 168 * h + L * x
+            if k == 7:
+                scan(oo[:, 4 + h, 0:84], oo[:, 2 + h, 5:89], d1[:, a:a + 168:2], D + "".join(" o%d1%d" % (j, h) for j in range(4)), "of" + H)
+            else:
+                scan(oo[quad(q + x), 2 * (1 - x) + h, 0:84], oo[quad(q), 2 * x + h, 5:89], d1[quad(q), a:a + 168:2],
+                     D + " o%d%d%d" % (q, x, h), "o%d%d%d" % (q + x, 1 - x, h))
+        elif c == "n":
+            vt(T.t1[:, h, :, 0:4], oo[:, 2 + h:6:2, 9:84:L], oo[:, 2 + h:6:2, 14:84:L], A.subtract,
+               "of" + H + "".join(" o%d1%d" % (j, h) for j in range(4)), "t1" + H)
+        elif c == "u":
+            turn(T["t2" + lh][:], T.t1[:, h], "t1" + H, "t2" + H)
+        elif c == "v":
+            for j in range(2):
+                turn(T.t3[:, h, j:64:2], T["t2" + lh][:, :, j, :], "t2" + H, "t3%d%d" % (h, j))
+        elif c == "w":
+            n = ("gl", "go")[h] + ts
+            vs(T[n][:], T.t3[:, h, 0:8], 512.0, 128.25, A.mult, "t3%d0 t3%d1" % (h, h), n, A.add)
+            if h:
+                send(T["ga" + ts][:], T[n][:], "g", t, n, "ga" + ts)
+                n = "ga" + ts
+            lists[h] = (T[n][:], n)
+        elif c == "z":
+            (vc if k < 2 else ac)(T["z" + lh + ts][:, k:512:4], T["f" + lh][:, 256 * k:256 * k + 256].indirect(lists[h][0]),
+                                  "f%s%d %s" % (lh, k, lists[h][1]), "z%s%s%d" % (lh, ts, k))
+        elif c == "q":
+            quant(T["q" + lh + ts][:], T["q" + lh + "s" + ts][:], T["z" + lh + ts][:], " ".join("z%s%s%d" % (lh, ts, j) for j in range(4)), "q" + lh + ts)
+        elif c == "r":
+            q, qs = T["q" + lh + ts], T["q" + lh + "s" + ts]
+            mm(bank, 128, T.lw[:, half(k)], T.lws[:, half(k)], q[:], qs[:], "lw q" + lh + ts, True, False)
+            mm(bank, 128, T.qe[:, half(k)], T.qes[:, half(k)], q[:], qs[:], "qe%d q" % k + lh + ts, False, True)
+        elif c in "xX":
+            xk = "x%s%d" % (lh, t + 1)
+            if c == "x":
+                vs(T[xk][:, k:512:4], T[bank][:, 0:128], 0.015625, None, A.mult, bank, "%s_%d" % (xk, k))
+            else:
+                ac(T[xk][:, k:512:4], T[bank][:, 0:128], bank, "%s_%d" % (xk, k), 0.015625)
+        elif c == "Q":
+            xk, key = "x%s%d" % (lh, t + 1), "qx%d%s" % (t + 1, name[1])
+            qn, qns = T["qx%d" % (t + 1)][:, half(h)], T["qxs%d" % (t + 1)]
+            quant(qn, qns[:, half(h)], T[xk][:], " ".join("%s_%d" % (xk, b) for b in range(4)), key)
+            if t < R - 1 and h:
+                send_state(t + 1)
+            if t == R - 1:
+                lst = [("y", T.oc[:, 512 * h:512 * h + 512], qn.bitcast(dt.uint8))]
+                lst += [("y", T.osc[4 * j:4 * j + 4, half(h)], qns[32 * j:32 * j + 4, half(h)]) for j in range(4)]
+                dmas("doc" + lh, lst, key, "")
+        elif c == "m":
+            if t < R - 1:
+                score_mm(t + 1, h)
+            else:
+                mm(bank, 128, T.qv[:], T.qvs[:], T.qx3[:, half(h)], T.qxs3[:, half(h)], "qv qx3" + name[1])
+        elif c == "y":
+            ac(T.ys[:, half(h)], T[bank][:, 0:128], bank, "ys" + H)
+            dmas("dy" + lh, [("s", T.y[:, half(h)], T.ys[:, half(h)])], "ys" + H, "")
+        elif c == "g":
+            if t < R - 1:
+                prefetch(h)
+            else:
+                ac(T.oaf[:, half(h)], T.idt[:].indirect(lists[h][0]), "idt " + lists[h][1], "oa" + H)
+        elif c == "V":
+            quant(T.qv[:], T.qvs[:], T.vt[:], "vt", "qv")
+        elif c == "O":
+            dmas("doa", [("y", T.oa[:], T.oaf[0:128:16, :])], "oa0 oa1", "")
 
     for t in range(R):
-        ts = "%d" % t
-        gl, go, ga = T["gl" + ts], T["go" + ts], T["ga" + ts]
-        score_bits(1)
-        if t == 0:
-            for b in range(1, 4):
-                quant(T.qe[:, half(b)], T.qes[:, half(b)], T.et[:, 512 * b:512 * b + 512], "et et_%d" % b, "qe%d" % b)
-        for n, bk, q, k in (("f", [1, 2, 3, 5], "qx", "qx%dL qx%dH" % (t, t)), ("fa", [6, 7, 0, 4], "qn", "qnc%d qns%d" % (t, t))):
-            for b in range(4):
-                mm(BANK[bk[b]], 256, T.qe[:, half(b)], T.qes[:, half(b)], T[q + ts][:], T[q + "s" + ts][:], "qe%d " % b + k)
-                ac(T[n][:, 256 * b:256 * b + 256], T[BANK[bk[b]]][:, 0:256], BANK[bk[b]], "%s_%d" % (n, b), 0.015625)
-
-        def pick(h):
-            vt(T.gm[:, half(h)], T.sb[:].indirect(lists[h][0]), T.pg[:, half(h)], A.mult, "sb0 sb1 pg%d %s" % (h, lists[h][1]), "gm%d" % h)
-
-        pick(1)
-        edge_turn(1)
-        pick(0)
-        edge_add(1)
-        turn(T.tb[:, half(1)], T.gm[:, half(1)], "gm1", "tb1")
-        edge_scan(1)
-        turn(T.tb[:, half(0)], T.gm[:, half(0)], "gm0", "tb0")
-        for k in range(5):
-            vt(d1[:, 10 + 2 * k:10 + 2 * k + 16 * L:L], T.tb[:, k:256:16], T.tb[:, 8 + k:256:16], A.add, "d1a d1b d1c tb0 tb1", "d%d" % k)
-        D = "oop d1a d1b d1c d0 d1 d2 d3 d4 "
-        for gr in range(8):
-            q, x = gr // 2, gr % 2
-            for h in (1, 0):
-                a = 168 * h + L * x
-                if gr == 7:
-                    scan(oo[:, 4 + h, 0:84], oo[:, 2 + h, 5:89], d1[:, a:a + 168:2], D + " ".join("o%d1%d" % (k, h) for k in range(4)), "of%d" % h)
-                else:
-                    scan(oo[quad(q + x), 2 * (1 - x) + h, 0:84], oo[quad(q), 2 * x + h, 5:89], d1[quad(q), a:a + 168:2],
-                         D + "o%d%d%d" % (q, x, h), "o%d%d%d" % (q + x, 1 - x, h))
-        vt(T.t1[:, :, 0:4], oo[:, 2:6, 9:84:L], oo[:, 2:6, 14:84:L], A.subtract,
-           "of0 of1 " + " ".join("o%d1%d" % (k, h) for k in range(4) for h in range(2)), "t1")
-        turn(T.t2[:], T.t1[:], "t1", "t2")
-        for c in range(2):
-            turn(T.t3[:, c:64:2], T.t2[:, :, c, :], "t2", "t3%d" % c)
-        vs(go[:], T.t3[:, 32:40], 512.0, 128.25, A.mult, "t30 t31", "go" + ts, A.add)
-        vs(gl[:], T.t3[:, 0:8], 512.0, 128.25, A.mult, "t30 t31", "gl" + ts, A.add)
-        send(ga[:], go[:], "g", t, "go" + ts, "ga" + ts)
-        lists = [(gl[:], "gl" + ts), (ga[:], "ga" + ts)]
-
-        def make_z(h):
-            k, n = "lh"[h] + ts, ("f", "fa")[h]
-            z = T["z" + k]
-            for b in range(4):
-                (vc if b < 2 else ac)(z[:, b:512:4], T[n][:, 256 * b:256 * b + 256].indirect(lists[h][0]), "%s_%d %s" % (n, b, lists[h][1]), "z%s_%d" % (k, b))
-            quant(T["q" + k][:], T["q" + "lh"[h] + "s" + ts][:], z[:], " ".join("z%s_%d" % (k, b) for b in range(4)), "q" + k)
-
-        def make_r(h):
-            q, qs, kk = T["q" + "lh"[h] + ts], T["q" + "lh"[h] + "s" + ts], "q" + "lh"[h] + ts
-            for b in range(4):
-                mm(BANK[4 * h + b], 128, T.lw[:, half(b)], T.lws[:, half(b)], q[:], qs[:], "lw " + kk, True, False)
-                mm(BANK[4 * h + b], 128, T.qe[:, half(b)], T.qes[:, half(b)], q[:], qs[:], "qe%d " % b + kk, False, True)
-
-        def make_x(h):
-            a, xk = half(h), "x%s%d" % ("lh"[h], t + 1)
-            for b in range(4):
-                bank = BANK[4 * h + b]
-                xo, xi, w = T[xk][:, b:512:4], T[bank][:, 0:128], "%s_%d" % (xk, b)
-                if b % 2:
-                    vs(xo, xi, 0.015625, None, A.mult, bank, w)
-                else:
-                    ac(xo, xi, bank, w, 0.015625)
-            qn, qns, key = T["qx%d" % (t + 1)], T["qxs%d" % (t + 1)], "qx%d%s" % (t + 1, "LH"[h])
-            quant(qn[:, a], qns[:, a], T[xk][:], " ".join("%s_%d" % (xk, b) for b in range(4)), key)
-            if t < R - 1:
-                return
-            mm(BANK[4 * h], 128, T.qv[:], T.qvs[:], qn[:, a], qns[:, a], "qv " + key)
-            lst = [("y", T.oc[:, 512 * h:512 * h + 512], qn[:, a].bitcast(dt.uint8))]
-            lst += [("y", T.osc[4 * k:4 * k + 4, a], qns[32 * k:32 * k + 4, a]) for k in range(4)]
-            dmas("doc" + "lh"[h], lst, key, "")
-            ac(T.ys[:, a], T[BANK[4 * h]][:, 0:128], BANK[4 * h], "ys%d" % h)
-            dmas("dy" + "lh"[h], [("s", T.y[:, a], T.ys[:, a])], "ys%d" % h, "")
-
-        def addresses(h):
-            ac(T.oaf[:, half(h)], T.idt[:].indirect(lists[h][0]), "idt " + lists[h][1], "oa%d" % h)
-
-        after = prefetch if t < R - 1 else lambda h, a, b: addresses(h)
-        make_z(0)
-        make_r(0)
-        after(0, *lists[0])
-        if t == R - 1:
-            quant(T.qv[:], T.qvs[:], T.vt[:], "vt", "qv")
-        make_x(0)
-        make_z(1)
-        if t < R - 1:
-            score_mm(t + 1, 0)
-        make_r(1)
-        after(1, *lists[1])
-        if t < R - 1:
-            score_bits(0)
-            edge_turn(0)
-            edge_add(0)
-            edge_scan(0)
-        else:
-            dmas("doa", [("y", T.oa[:], T.oaf[0:128:16, :])], "oa0 oa1", "")
-        make_x(1)
-        if t < R - 1:
-            send_state(t + 1)
-            score_mm(t + 1, 1)
+        for name in " ".join((NEXT if t else FIRST, CARRY, STATE if t < R - 1 else LAST)).split():
+            step(t, name)
     for s in sorted(cnt):
         if known["g"].get(s, 0) < cnt[s]:
             g.wait_ge(T.sem[s], cnt[s])

@@ -8,11 +8,10 @@ BIG = 1.5 * 2.0 ** 23
 SCRATCH = {}
 for _d, _l in (
         ("int32", "nxi:128 nt:128 ali:16 i16:8"),
-        ("float32", "uu:16,5,16 tab:256 cs:8,16 ct:8,16 jj:176 d1:360 ini:176 oo:6,105 pg:256 gm:256 tb:256 "
+        ("float32", "uu:16,5,16 tab:256 cs:8,16 ct:8,16 pat:8,21 d1:360 ini:168 oo:6,84 pg:256 gm:256 tb:256 "
                     "t1:2,2,32 t2l:2,2,16 t2h:2,2,16 t3:2,64 idt:256 oaf:256 ys:256"),
-        ("bfloat16", "i64:128 c64:128 et:2048 ut:512 vt:512 sb:256 eg:256 fl:1024 fh:1024 "
-                     "xl0:512 xl1:512 xl2:512 xl3:512 xh0:512 xh1:512 xh2:512 xh3:512 "
-                     "zl0:512 zl1:512 zl2:512 zh0:512 zh1:512 zh2:512"),
+        ("bfloat16", "i64:128 c64:128 et:2048 ut:512 vt:512 sb:256 eg:256 fl:1024 fh:1024 x0:1024 "
+                     "xl1:512 xl2:512 xl3:512 xh1:512 xh2:512 xh3:512 zl0:512 zl1:512 zl2:512 zh0:512 zh1:512 zh2:512"),
         ("uint16", "ul:8 g0:16 gl0:8 gl1:8 gl2:8 go0:8 go1:8 go2:8 ga0:8 ga1:8 ga2:8")):
     for _s in _l.split():
         SCRATCH[_s.split(":")[0]] = ("sbuf", [128] + [int(k) for k in _s.split(":")[1].split(",")], _d)
@@ -24,16 +23,15 @@ for _s in "qe:512 lw:512 qu:128 qy:128 qv:128 qx:256:4 qh:128:3 ql:128:3 qn:256:
 BANK = ["b%d" % k for k in range(10, 18)]
 for _s in BANK:
     SCRATCH[_s] = ("psum", [128, 512], "float32")
-SEMAPHORES = ("cv cs ct cg dnx dal dxl dxh du dv dw dyl dyh doa docl doch".split()
+SEMAPHORES = ("cv cs ct cg dnx dal dx du dv dw dyl dyh doa docl doch".split()
               + [n + "%d" % t for n in ("rc", "lc", "rs", "ls", "rg", "lg") for t in range(R)])
-FIRST = "bL eL bH aL iL"
-NEXT = "bH iL"
-CARRY = ("pH eH fL0 fL1 fL2 tH DH aH dH0 dH1 iH dH2 dH3 fL3 pL sH0 tL DL sH1 dL0 dL1 sH2 dL2 dL3 fH0 fH1 fH2 fH3 "
-         "sH3 sL0 sH4 sL1 sH5 sL2 sH6 sL3 sH7 sL4 nH sL5 uH sL6 vH sL7 wH nL uL vL wL")
-STATE = ("zL0 zL1 zL2 zL3 qL rL0 rL1 rL2 rL3 gL zH0 zH1 zH2 zH3 qH rH0 rH1 rH2 rH3 XL0 xL1 XL2 xL3 QL mL "
-         "XH0 xH1 XH2 xH3 gH bL QH mH eL aL")
-LAST = ("zL0 zL1 zL2 zL3 qL rL0 rL1 rL2 rL3 VL gL zH0 zH1 zH2 zH3 qH rH0 rH1 rH2 rH3 XL0 xL1 XL2 xL3 QL mL "
-        "XH0 xH1 XH2 xH3 QH mH gH OL yL yH")
+FIRST = ("TL0 TL1 bH TL2 bL TL3 GH GL eH eL aH aL PH iH PL iL fL0 fL1 tH tL JL jL0 jL1 jL2 jL3 fL2 fL3 fH0 fH1 fH2 fH3 "
+         + " ".join("sH%d sL%d" % (k, k) for k in range(8)) + " nH nL uH uL vH vL wH wL")
+CARRY = ("bH iL pH eH pL fL0 fL1 fL2 tH DH aH tL DL dH0 dH1 dH2 dH3 iH fL3 dL0 dL1 sH0 dL2 dL3 sH1 fH0 fH1 fH2 fH3 "
+         + " ".join("sL%d sH%d" % (k, k + 2) for k in range(6)) + " sL6 nH sL7 uH nL vH uL wH vL wL")
+STATE = "zL0 zL1 zL2 zL3 qL rL0 rL1 rL2 rL3 VL zH0 zH1 zH2 zH3 qH rH0 rH1 rH2 rH3 XL0 xL1 XL2 xL3 gL QL mL XH0 xH1 XH2 xH3 gH"
+NEXT = "bL QH mH eL aL"
+LAST = "OL yL QH mH yH"
 
 
 def rank_program(g, core, T, topo):
@@ -157,14 +155,12 @@ def rank_program(g, core, T, topo):
     dmas("dnx", [("y", T.nxi[:], T.nx[:])], "", "nxi")
     dmas("dal", [("s", T.ali[:], T.al[:])], "", "ali")
     dmas("du", [("y", T.ut[:], T.u[:])], "", "ut")
-    dmas("dxh", [("s", T.xh0[:], T.x[:, 512:1024])], "", "xh0")
-    dmas("dxl", [("y", T.xl0[:], T.x[:, 0:512])], "", "xl0")
-    dmas("dw", [("y", T.lw[:].bitcast(dt.uint8), T.wc[:]), ("y", T.lws[:], T.ws[:])], "xl0 xh0", "lw")
+    dmas("dx", [("y", T.x0[:], T.x[:])], "", "x0")
+    dmas("dw", [("y", T.lw[:].bitcast(dt.uint8), T.wc[:]), ("y", T.lws[:], T.ws[:])], "x0", "lw")
     dmas("dv", [("y", T.vt[:], T.v[:])], "", "vt")
 
     fill(T.c64[:], 64.0, "c64")
     fill(T.et[:], 0.0, "et")
-    iota(T.jj[:, 0:168], [[0, 8], [1, L]], 0, 0, "jj")
     op("g", lambda: g.affine_select(T.i64[:], T.c64[:], [[-1, 128]], A.is_equal, 0.0, 0, 1), "c64", "i64")
     op("g", lambda: g.iota(T.i16[:], [[16, 8]], 0, 0), "", "i16")
     for q in range(4):
@@ -178,22 +174,14 @@ def rank_program(g, core, T, topo):
     for b in range(4):
         ac(T.et[:, 512 * b + b:512 * b + 512:4], T.i64[:], "i64 et", "et_%d" % b)
     turn(T.ct[:], cs[:], " ".join("cs%d" % k for k in range(len(slots))), "ct")
-    vs(T.ini[:, 0:167], T.jj[:, 1:168], 13.0, None, A.is_ge, "jj", "ini")
+    fill(uu[:, :, 0, 4:8], 0.0, "u0")
     vs(T.ul[:], T.i16[:], bit, None, A.add, "i16 ct", "ul")
     for b in range(4):
         quant(T.qe[:, half(b)], T.qes[:, half(b)], T.et[:, 512 * b:512 * b + 512], "et et_%d" % b, "qe%d" % b)
-    const(uu[:, :, 0, 4:8], 64, 0.0, "u0")
     const(uu[:, :, 0, 14:16], 32, 0.0, "u1")
-    const(T.ini[:, 167:176], 9, 0.0, "inp")
-    const(T.t1[:], 128, 0.0, "t10 t11")
-    const(oo[:, :, 84:105], 126, 0.0, "oop")
-    ac(d1[:, 0:336:2], T.ini[:, 0:168], "ini inp", "d1a")
-    ac(d1[:, L:L + 336:2], T.ini[:, 0:168], "ini inp", "d1b")
-    UA = "u0 u1 ua0 ua1 ua2 ua3 "
-    op("s", lambda: S.activation(uu[:, :, 0, 12], uu[:, :, 0, 13], AF.Identity, bias=-128.0), UA, "u12")
-    const(T.ini[:, 10:168:L], 8, -2.0, "ini inp")
-    const(d1[:, 20:20 + 16 * L:L], 16, BIG, "d1a d1b")
-    const(d1[:, 22:22 + 16 * L:L], 16, -BIG - 3.0, "d1a d1b d1c")
+    for a, b, val in ((0, 10, 0.0), (10, 11, BIG), (11, 12, -BIG - 3.0), (12, 20, 1.0), (20, 21, 0.0)):
+        const(T.pat[:, :, a:b], 8 * (b - a), val, "pat%d" % a)
+    UA, PAT = "u0 u1 ua0 ua1 ua2 ua3 ", "pat0 pat10 pat11 pat12 pat20"
 
     def score_mm(t, h):
         mm(BANK[4 * h], 128, T.qy[:], T.qys[:], T["qx%d" % t][:, half(h)], T["qxs%d" % t][:, half(h)], "qy qys qx%d" % t + "LH"[h])
@@ -203,9 +191,6 @@ def rank_program(g, core, T, topo):
         send(T["qn%d" % t][:].bitcast(dt.uint8), T["qx%d" % t][:].bitcast(dt.uint8), "c", t, k, "qnc%d" % t)
         send(T["qns%d" % t][:], T["qxs%d" % t][:], "s", t, k, "qns%d" % t)
 
-    def prefetch(h):
-        ac(T.pg[:, half(h)], T.tab[:].indirect(lists[h][0]), "ct tab0 tab1 tab2 tab3 " + lists[h][1], "pg%d" % h, scl)
-
     def level(k):
         src = slice(5 - k if k > 1 else 5, 16, 8)
         vt(uu[:, :, 0:5 - k, 4 - k:16:8], uu[:, :, 1:6 - k, src], uu[:, :, 0:5 - k, src], A.subtract,
@@ -214,58 +199,73 @@ def rank_program(g, core, T, topo):
     lists = [(T.g0[:, 0:8], "g0"), (T.g0[:, 8:16], "g0")]
     turn(T.nt[:], T.nxi[:], "nxi", "nt")
     vc(T.g0[:], T.ali[:], "ali", "g0")
-    vc(uu[:, :, 1:5, 13], T.nt[:, 0:64], "nt", "y0")
+    ac(uu[:, :, 1:5, 13], T.nt[:, 0:64], "nt", "y0")
     vt(uu[:, :, 1:5, 5], T.nt[:, 64:128], T.nt[:, 0:64], A.subtract, "nt", "y1")
-    quant(T.qu[:], T.qus[:], T.ut[:], "ut", "qu")
+    op("s", lambda: S.activation(uu[:, :, 0, 12], uu[:, :, 0, 13], AF.Identity, bias=-128.0), UA, "u12")
+    ac(T.ini[:], T.pat[:], PAT, "ini")
+    ac(d1[:, 0:336:2], T.pat[:], PAT, "d1a")
+    ac(d1[:, L:L + 336:2], T.pat[:], PAT, "d1b")
     level(1)
+    quant(T.qu[:], T.qus[:], T.ut[:], "ut", "qu")
+    level(2)
     vc(T.qy[:].bitcast(dt.uint32), T.qu[:].bitcast(dt.uint32).indirect(T.ul[:]), "qu ul", "qy")
     ac(T.qys[:], T.qus[:].indirect(T.ul[:]), "qu ul", "qys")
-    level(2)
-    quant(T.qx0[:, 128:256], T.qxs0[:, 128:256], T.xh0[:], "xh0", "qx0H")
+    const(T.ini[:, 10:168:L], 8, -2.0, "ini")
+    const(T.t1[:], 128, 0.0, "t10 t11")
+    const(oo[:, :, 78:83], 30, 1.0, "oop")
     level(3)
-    quant(T.qx0[:, 0:128], T.qxs0[:, 0:128], T.xl0[:], "xl0", "qx0L")
-    score_mm(0, 0)
+    quant(T.qx0[:, 128:256], T.qxs0[:, 128:256], T.x0[:, 512:1024], "x0", "qx0H")
     score_mm(0, 1)
-    send_state(0)
     level(4)
-    for m in range(4):
-        turn(T.tab[:, m:256:4], uu[:, m:16:4, 0, :], UA + "u12 lv1 lv2 lv3 lv4", "tab%d" % m)
-    prefetch(1)
-    prefetch(0)
+    quant(T.qx0[:, 0:128], T.qxs0[:, 0:128], T.x0[:, 0:512], "x0", "qx0L")
+    score_mm(0, 0)
+    send_state(0)
+    TAB = "tab0 tab1 tab2 tab3 "
 
     def step(t, name):
         c, h, k = name[0], "LH".index(name[1]), int(name[2:] or 0)
         ts, H, lh = "%d" % t, "%d" % h, "lh"[h]
         a, bank = 128 * h, BANK[4 * h + k % 4]
-        if c == "b":
+        lst, lk = lists[h]
+        if c == "T":
+            turn(T.tab[:, k:256:4], uu[:, k:16:4, 0, :], UA + "u12 lv1 lv2 lv3 lv4", "tab%d" % k)
+        elif c == "b":
             vs(T.sb[:, half(h)], T[bank][:, 0:128], thr, mul, A.is_gt, "ct " + bank, "sb" + H, A.mult)
         elif c == "e":
             turn(T.eg[0:32, half(h)], T.sb[0:32, half(h)], "sb" + H, "eg" + H)
         elif c == "a":
             vt(T.ini[0:32, 84 * h + 11:84 * h + 84:L], T.eg[0:32, a + 4:a + 128:32], T.eg[0:32, a + 20:a + 128:32], A.add, "ini eg" + H, "in" + H)
         elif c == "i":
-            scan(oo[0:32, h, 0:84], T.ini[0:32, 84 * h + 5:84 * h + 89], T.ini[0:32, 84 * h:84 * h + 84], "ini inp in" + H, "o00" + H)
+            scan(oo[0:32, h, 10:78], T.ini[0:32, 84 * h + 15:84 * h + 83], T.ini[0:32, 84 * h + 10:84 * h + 78], "ini in" + H, "o00" + H)
         elif c == "f":
             bank, q = BANK[[[1, 2, 3, 5], [6, 7, 0, 4]][h][k]], ("qx", "qn")[h]
             mm(bank, 256, T.qe[:, half(k)], T.qes[:, half(k)], T[q + ts][:], T[q + "s" + ts][:],
                "qe%d " % k + ("qx%sL qx%sH", "qnc%s qns%s")[h] % (ts, ts))
             ac(T["f" + lh][:, 256 * k:256 * k + 256], T[bank][:, 0:256], bank, "f%s%d" % (lh, k), 0.015625)
         elif c == "p":
-            vt(T.gm[:, half(h)], T.sb[:].indirect(lists[h][0]), T.pg[:, half(h)], A.mult, "sb0 sb1 pg%d %s" % (h, lists[h][1]), "gm" + H)
+            vt(T.gm[:, half(h)], T.sb[:].indirect(lst), T.pg[:, half(h)], A.mult, "sb0 sb1 pg%d %s" % (h, lk), "gm" + H)
+        elif c == "G":
+            ac(T.pg[:, half(h)], T.sb[:].indirect(lst), "ct sb0 sb1 " + lk, "pg" + H, scl)
+        elif c == "P":
+            vt(T.gm[:, half(h)], T.tab[:].indirect(lst), T.pg[:, half(h)], A.mult, TAB + "pg%d %s" % (h, lk), "gm" + H)
         elif c == "t":
             turn(T.tb[:, half(h)], T.gm[:, half(h)], "gm" + H, "tb" + H)
         elif c == "d":
             vt(d1[:, 168 * h + 10 + 2 * k:168 * h + 168:L], T.tb[:, a + k:a + 128:16], T.tb[:, a + 8 + k:a + 128:16], A.add,
-               "d1a d1b d1c tb" + H, "d%d%d" % (h, k))
+               "d1a d1b tb" + H, "d%d%d" % (h, k))
         elif c == "D":
-            ac(d1[:, 168 * h + 18:168 * h + 168:L], T.tb[:, a + 12:a + 128:16], "d1a d1b d1c tb" + H, "d%d4" % h)
+            ac(d1[:, 168 * h + 18:168 * h + 168:L], T.tb[:, a + 12:a + 128:16], "d1a d1b tb" + H, "d%d4" % h)
+        elif c == "j":
+            vt(d1[:, 10 + 2 * k:336:L], T.tb[:, k:256:16], T.tb[:, 8 + k:256:16], A.add, "d1a d1b tb0 tb1", "d0%d d1%d" % (k, k))
+        elif c == "J":
+            ac(d1[:, 18:336:L], T.tb[:, 12:256:16], "d1a d1b tb0 tb1", "d04 d14")
         elif c == "s":
             q, x = k // 2, k % 2
-            D, a = "oop d1a d1b d1c " + " ".join("d%d%d" % (h, j) for j in range(5)), 168 * h + L * x
+            D, a = "oop d1a d1b " + " ".join("d%d%d" % (h, j) for j in range(5)), 168 * h + L * x
             if k == 7:
-                scan(oo[:, 4 + h, 0:84], oo[:, 2 + h, 5:89], d1[:, a:a + 168:2], D + "".join(" o%d1%d" % (j, h) for j in range(4)), "of" + H)
+                scan(oo[:, 4 + h, 5:78], oo[:, 2 + h, 10:83], d1[:, a + 10:a + 156:2], D + "".join(" o%d1%d" % (j, h) for j in range(4)), "of" + H)
             else:
-                scan(oo[quad(q + x), 2 * (1 - x) + h, 0:84], oo[quad(q), 2 * x + h, 5:89], d1[quad(q), a:a + 168:2],
+                scan(oo[quad(q + x), 2 * (1 - x) + h, 5:78], oo[quad(q), 2 * x + h, 10:83], d1[quad(q), a + 10:a + 156:2],
                      D + " o%d%d%d" % (q, x, h), "o%d%d%d" % (q + x, 1 - x, h))
         elif c == "n":
             vt(T.t1[:, h, :, 0:4], oo[:, 2 + h:6:2, 9:84:L], oo[:, 2 + h:6:2, 14:84:L], A.subtract,
@@ -283,8 +283,8 @@ def rank_program(g, core, T, topo):
                 n = "ga" + ts
             lists[h] = (T[n][:], n)
         elif c == "z":
-            (vc if k < 2 else ac)(T["z" + lh + ts][:, k:512:4], T["f" + lh][:, 256 * k:256 * k + 256].indirect(lists[h][0]),
-                                  "f%s%d %s" % (lh, k, lists[h][1]), "z%s%s%d" % (lh, ts, k))
+            (vc if k < 2 else ac)(T["z" + lh + ts][:, k:512:4], T["f" + lh][:, 256 * k:256 * k + 256].indirect(lst),
+                                  "f%s%d %s" % (lh, k, lk), "z%s%s%d" % (lh, ts, k))
         elif c == "q":
             quant(T["q" + lh + ts][:], T["q" + lh + "s" + ts][:], T["z" + lh + ts][:], " ".join("z%s%s%d" % (lh, ts, j) for j in range(4)), "q" + lh + ts)
         elif c == "r":
@@ -304,29 +304,29 @@ def rank_program(g, core, T, topo):
             if t < R - 1 and h:
                 send_state(t + 1)
             if t == R - 1:
-                lst = [("y", T.oc[:, 512 * h:512 * h + 512], qn.bitcast(dt.uint8))]
-                lst += [("y", T.osc[4 * j:4 * j + 4, half(h)], qns[32 * j:32 * j + 4, half(h)]) for j in range(4)]
-                dmas("doc" + lh, lst, key, "")
+                out = [("y", T.oc[:, 512 * h:512 * h + 512], qn.bitcast(dt.uint8))]
+                out += [("ys"[h * (j // 2)], T.osc[4 * j:4 * j + 4, half(h)], qns[32 * j:32 * j + 4, half(h)]) for j in range(4)]
+                dmas("doc" + lh, out, key, "")
         elif c == "m":
             if t < R - 1:
                 score_mm(t + 1, h)
             else:
                 mm(bank, 128, T.qv[:], T.qvs[:], T.qx3[:, half(h)], T.qxs3[:, half(h)], "qv qx3" + name[1])
         elif c == "y":
-            ac(T.ys[:, half(h)], T[bank][:, 0:128], bank, "ys" + H)
+            (vc if h else ac)(T.ys[:, half(h)], T[bank][:, 0:128], bank, "ys" + H)
             dmas("dy" + lh, [("s", T.y[:, half(h)], T.ys[:, half(h)])], "ys" + H, "")
         elif c == "g":
             if t < R - 1:
-                prefetch(h)
+                ac(T.pg[:, half(h)], T.tab[:].indirect(lst), "ct " + TAB + lk, "pg" + H, scl)
             else:
-                ac(T.oaf[:, half(h)], T.idt[:].indirect(lists[h][0]), "idt " + lists[h][1], "oa" + H)
-        elif c == "V":
+                ac(T.oaf[:, half(h)], T.idt[:].indirect(lst), "idt " + lk, "oa" + H)
+        elif c == "V" and t == 0:
             quant(T.qv[:], T.qvs[:], T.vt[:], "vt", "qv")
         elif c == "O":
             dmas("doa", [("y", T.oa[:], T.oaf[0:128:16, :])], "oa0 oa1", "")
 
     for t in range(R):
-        for name in " ".join((NEXT if t else FIRST, CARRY, STATE if t < R - 1 else LAST)).split():
+        for name in " ".join((CARRY if t else FIRST, STATE, NEXT if t < R - 1 else LAST)).split():
             step(t, name)
     for s in sorted(cnt):
         if known["g"].get(s, 0) < cnt[s]:

@@ -7,10 +7,10 @@ L = 21
 BIG = 1.5 * 2.0 ** 23
 SCRATCH = {}
 for _d, _l in (
-        ("int32", "nxi:128 nt:128 ali:16 i16:8"),
-        ("float32", "uu:16,5,16 tab:256 cs:8,16 ct:8,16 pat:8,21 d1:360 ini:168 oo:6,84 pg:256 gm:256 tb:256 "
+        ("int32", "nxi:128 yy:16,5,2 ali:16"),
+        ("float32", "uu:16,5,16 tab:256 cs:10,16 ct:10,16 am:16 pat:8,21 i16:8 d1:360 ini:168 oo:6,84 pg:256 gm:256 tb:256 "
                     "t1:2,2,32 t2l:2,2,16 t2h:2,2,16 t3:2,64 idt:256 oaf:256 ys:256"),
-        ("bfloat16", "i64:128 c64:128 et:2048 ut:512 vt:512 sb:256 eg:256 fl:1024 fh:1024 x0:1024 "
+        ("bfloat16", "i64:128 c64:128 et:516 ut:512 vt:512 sb:256 eg:6112 fl:1024 fh:1024 x0:1024 "
                      "xl1:512 xl2:512 xl3:512 xh1:512 xh2:512 xh3:512 zl0:512 zl1:512 zl2:512 zh0:512 zh1:512 zh2:512"),
         ("uint16", "ul:8 g0:16 gl0:8 gl1:8 gl2:8 go0:8 go1:8 go2:8 ga0:8 ga1:8 ga2:8")):
     for _s in _l.split():
@@ -25,12 +25,11 @@ for _s in BANK:
     SCRATCH[_s] = ("psum", [128, 512], "float32")
 SEMAPHORES = ("cv cs ct cg dnx dal dx du dv dw dyl dyh doa docl doch".split()
               + [n + "%d" % t for n in ("rc", "lc", "rs", "ls", "rg", "lg") for t in range(R)])
-FIRST = ("TL0 TL1 bH TL2 bL TL3 GH GL eH eL aH aL PH iH PL iL fL0 fL1 tH tL JL jL0 jL1 jL2 jL3 fL2 fL3 fH0 fH1 fH2 fH3 "
-         + " ".join("sH%d sL%d" % (k, k) for k in range(8)) + " nH nL uH uL vH vL wH wL")
-CARRY = ("bH iL pH eH pL fL0 fL1 fL2 tH DH aH tL DL dH0 dH1 dH2 dH3 iH fL3 dL0 dL1 sH0 dL2 dL3 sH1 fH0 fH1 fH2 fH3 "
-         + " ".join("sL%d sH%d" % (k, k + 2) for k in range(6)) + " sL6 nH sL7 uH nL vH uL wH vL wL")
-STATE = "zL0 zL1 zL2 zL3 qL rL0 rL1 rL2 rL3 VL zH0 zH1 zH2 zH3 qH rH0 rH1 rH2 rH3 XL0 xL1 XL2 xL3 gL QL mL XH0 xH1 XH2 xH3 gH"
-NEXT = "bL QH mH eL aL"
+FIRST = "bH TL0 TL1 bL GH GL TL2 TL3 eH EL1 eL EL2 PH PL fL0 fL1 tH iH tL iL JL jL0 jL1 jL2 jL3 EL3 fL2"
+SIGNS = "bH iL pH pL fL0 fL1 fL2 tH eH tL JL iH jL0 jL1 jL2 jL3"
+CARRY = "fL3 fH0 fH1 fH2 fH3 " + " ".join("sH%d sL%d" % (k, k) for k in range(8)) + " nH nL uH uL vH vL wH wL"
+STATE = "VL zL0 zL1 zL2 zL3 qL rL0 rL1 rL2 rL3 zH0 zH1 zH2 zH3 qH rH0 rH1 rH2 rH3 XL0 xL1 XL2 xL3 gL QL mL XH0 xH1 XH2 xH3 gH"
+NEXT = "bL QH mH eL"
 LAST = "OL yL QH mH yH"
 
 
@@ -151,7 +150,7 @@ def rank_program(g, core, T, topo):
         return slice(32 * q, 32 * q + 32)
 
     uu, cs, d1, oo = T.uu, T.cs, T.d1, T.oo
-    thr, bit, mul, scl = [T.ct[:, 2 * k, 0:1] for k in range(4)]
+    thr, bit, less, scl, r4 = [T.ct[:, 2 * k, 0:1] for k in range(5)]
     dmas("dnx", [("y", T.nxi[:], T.nx[:])], "", "nxi")
     dmas("dal", [("s", T.ali[:], T.al[:])], "", "ali")
     dmas("du", [("y", T.ut[:], T.u[:])], "", "ut")
@@ -160,28 +159,35 @@ def rank_program(g, core, T, topo):
     dmas("dv", [("y", T.vt[:], T.v[:])], "", "vt")
 
     fill(T.c64[:], 64.0, "c64")
-    fill(T.et[:], 0.0, "et")
+    iota(cs[:, 8:10, :], [[4, 32]], 0, 0, "r4")
+    iota(T.am[:], [[128, 2], [0, 2], [1, 4]], 0, 0, "am")
     op("g", lambda: g.affine_select(T.i64[:], T.c64[:], [[-1, 128]], A.is_equal, 0.0, 0, 1), "c64", "i64")
-    op("g", lambda: g.iota(T.i16[:], [[16, 8]], 0, 0), "", "i16")
-    for q in range(4):
-        iota(uu[quad(q), :, 0, 13], [[128, 2], [0, 2], [1, 4]], 0, 4, "ua%d" % q)
     iota(T.idt[:], [[1, 256]], 0, 0, "idt")
-    slots = [(0, 4, 0, 4, 1, 0.0), (0, 2, 4, 8, 1, 0.0), (0, 2, 8, 16, 1, -1e29), (2, 6, 8, 16, 1, 1.0), (2, 4, 4, 8, 1, 1.0),
-             (4, 6, 0, 4, 1, 1.0), (4, 5, 4, 8, 1, 2.0), (5, 6, 4, 8, 1, 1.0), (6, 8, 4, 8, 1, 1.0), (6, 8, 11, 16, 1, 2.0 ** -9)]
-    slots += [(6, 8, k, 11 if k == 3 else 16, 8, 2.0 ** -9 / f) for k, f in enumerate((24, 6, 2, 1))]
+    slots = [(0, 6, 0, 4, 1, 0.0), (0, 2, 4, 12, 1, 0.0), (0, 2, 12, 16, 1, -1e29), (2, 4, 4, 8, 1, 1.0), (2, 4, 8, 12, 1, 0.0),
+             (4, 6, 4, 8, 1, 0.0), (4, 6, 8, 12, 1, 1.0), (2, 6, 12, 16, 1, 0.0), (6, 8, 4, 8, 1, 1.0), (6, 8, 12, 16, 1, 2.0 ** -9)]
+    slots += [(6, 8, k, 16, 8, 2.0 ** -9 / f) for k, f in enumerate((24, 6, 2, 1))]
     for k, (a, b, c, d, e, val) in enumerate(slots):
-        const(cs[:, a:b, c:d:e], (b - a) * len(range(c, d, e)), val, "cs%d" % k)
-    for b in range(4):
-        ac(T.et[:, 512 * b + b:512 * b + 512:4], T.i64[:], "i64 et", "et_%d" % b)
-    turn(T.ct[:], cs[:], " ".join("cs%d" % k for k in range(len(slots))), "ct")
-    fill(uu[:, :, 0, 4:8], 0.0, "u0")
-    vs(T.ul[:], T.i16[:], bit, None, A.add, "i16 ct", "ul")
-    for b in range(4):
-        quant(T.qe[:, half(b)], T.qes[:, half(b)], T.et[:, 512 * b:512 * b + 512], "et et_%d" % b, "qe%d" % b)
-    const(uu[:, :, 0, 14:16], 32, 0.0, "u1")
+        if k % 3:
+            fill(cs[:, a:b, c:d:e], val, "cs%d" % k)
+        else:
+            const(cs[:, a:b, c:d:e], (b - a) * len(range(c, d, e)), val, "cs%d" % k)
+    op("v", lambda: V.tensor_tensor_scan(T.i16[:], T.c64[:, 0:8], T.c64[:, 0:8], -128.0, A.add, A.add), "c64", "i16")
+    turn(T.ct[:], cs[:], " ".join("cs%d" % k for k in range(len(slots))) + " r4", "ct")
+    fill(T.et[:], 0.0, "et")
+    const(uu[:, :, 0, 4:8], 64, 0.0, "u0")
+
+    def unpacker(b):
+        quant(T.qe[:, half(b)], T.qes[:, half(b)], T.et[:, 3 - b:515 - b], "et", "qe%d" % b)
+
+    for b in range(2):
+        vs(T.yy[:, :, 0, b], T.am[:], r4, None, A.add, "am ct", "ua%d" % b)
+    vs(uu[:, :, 0, 12], T.am[:], r4, -128.0, A.add, "am ct", "u12", A.add)
+    vs(T.ul[:], T.i16[:], 0.125, bit, A.mult, "i16 ct", "ul", A.add)
+    const(uu[:, :, 0, 13:16], 48, 0.0, "u1")
     for a, b, val in ((0, 10, 0.0), (10, 11, BIG), (11, 12, -BIG - 3.0), (12, 20, 1.0), (20, 21, 0.0)):
         const(T.pat[:, :, a:b], 8 * (b - a), val, "pat%d" % a)
-    UA, PAT = "u0 u1 ua0 ua1 ua2 ua3 ", "pat0 pat10 pat11 pat12 pat20"
+    ac(T.et[:, 3:515:4], T.i64[:], "i64 et", "et")
+    UA, PAT = "u0 u1 ua0 ua1 ", "pat0 pat10 pat11 pat12 pat20"
 
     def score_mm(t, h):
         mm(BANK[4 * h], 128, T.qy[:], T.qys[:], T["qx%d" % t][:, half(h)], T["qxs%d" % t][:, half(h)], "qy qys qx%d" % t + "LH"[h])
@@ -192,34 +198,37 @@ def rank_program(g, core, T, topo):
         send(T["qns%d" % t][:], T["qxs%d" % t][:], "s", t, k, "qns%d" % t)
 
     def level(k):
-        src = slice(5 - k if k > 1 else 5, 16, 8)
-        vt(uu[:, :, 0:5 - k, 4 - k:16:8], uu[:, :, 1:6 - k, src], uu[:, :, 0:5 - k, src], A.subtract,
+        src, s = (uu, slice(5 - k, 16, 8)) if k > 1 else (T.yy, slice(0, 2))
+        vt(uu[:, :, 0:5 - k, 4 - k:12:8], src[:, :, 1:6 - k, s], src[:, :, 0:5 - k, s], A.subtract,
            UA + "y0 y1" if k == 1 else "lv%d" % (k - 1), "lv%d" % k)
 
     lists = [(T.g0[:, 0:8], "g0"), (T.g0[:, 8:16], "g0")]
-    turn(T.nt[:], T.nxi[:], "nxi", "nt")
     vc(T.g0[:], T.ali[:], "ali", "g0")
-    ac(uu[:, :, 1:5, 13], T.nt[:, 0:64], "nt", "y0")
-    vt(uu[:, :, 1:5, 5], T.nt[:, 64:128], T.nt[:, 0:64], A.subtract, "nt", "y1")
-    op("s", lambda: S.activation(uu[:, :, 0, 12], uu[:, :, 0, 13], AF.Identity, bias=-128.0), UA, "u12")
+    for b in range(2):
+        turn(T.yy[:, :, 1:5, 1 - b], T.nxi[:, 64 * b:64 * b + 64], "nxi", "y%d" % b)
     ac(T.ini[:], T.pat[:], PAT, "ini")
     ac(d1[:, 0:336:2], T.pat[:], PAT, "d1a")
     ac(d1[:, L:L + 336:2], T.pat[:], PAT, "d1b")
+    unpacker(0)
     level(1)
     quant(T.qu[:], T.qus[:], T.ut[:], "ut", "qu")
     level(2)
     vc(T.qy[:].bitcast(dt.uint32), T.qu[:].bitcast(dt.uint32).indirect(T.ul[:]), "qu ul", "qy")
     ac(T.qys[:], T.qus[:].indirect(T.ul[:]), "qu ul", "qys")
-    const(T.ini[:, 10:168:L], 8, -2.0, "ini")
+    MUL, ADD, EDGE = 400, 736, 636
+    ac(T.eg[:, ADD:ADD + 32 * 168:32], T.pat[:], PAT, "ea")
+    ac(T.eg[:, MUL:MUL + 32 * 163:32], T.ini[:, 5:168], "ini", "eb")
+    const(T.eg[:, ADD + 32 * 9:6112:32 * L], 8, 2.0, "ea")
+    const(T.eg[:, ADD + 32 * 11:6112:32 * L], 8, -2.0, "ea ec")
     const(T.t1[:], 128, 0.0, "t10 t11")
     const(oo[:, :, 78:83], 30, 1.0, "oop")
-    level(3)
     quant(T.qx0[:, 128:256], T.qxs0[:, 128:256], T.x0[:, 512:1024], "x0", "qx0H")
     score_mm(0, 1)
-    level(4)
+    level(3)
     quant(T.qx0[:, 0:128], T.qxs0[:, 0:128], T.x0[:, 0:512], "x0", "qx0L")
     score_mm(0, 0)
     send_state(0)
+    level(4)
     TAB = "tab0 tab1 tab2 tab3 "
 
     def step(t, name):
@@ -229,14 +238,15 @@ def rank_program(g, core, T, topo):
         lst, lk = lists[h]
         if c == "T":
             turn(T.tab[:, k:256:4], uu[:, k:16:4, 0, :], UA + "u12 lv1 lv2 lv3 lv4", "tab%d" % k)
+        elif c == "E":
+            unpacker(k)
         elif c == "b":
-            vs(T.sb[:, half(h)], T[bank][:, 0:128], thr, mul, A.is_gt, "ct " + bank, "sb" + H, A.mult)
+            vs(T.sb[:, half(h)], T[bank][:, 0:128], thr, less, A.is_gt, "ct " + bank, "sb" + H, A.subtract)
         elif c == "e":
-            turn(T.eg[0:32, half(h)], T.sb[0:32, half(h)], "sb" + H, "eg" + H)
-        elif c == "a":
-            vt(T.ini[0:32, 84 * h + 11:84 * h + 84:L], T.eg[0:32, a + 4:a + 128:32], T.eg[0:32, a + 20:a + 128:32], A.add, "ini eg" + H, "in" + H)
+            turn(T.eg[0:32, EDGE + L * a:EDGE + L * (a + 128):L], T.sb[0:32, half(h)], "ea eb ec sb" + H, "eg" + H)
         elif c == "i":
-            scan(oo[0:32, h, 10:78], T.ini[0:32, 84 * h + 15:84 * h + 83], T.ini[0:32, 84 * h + 10:84 * h + 78], "ini in" + H, "o00" + H)
+            a = L * a + 32 * 9
+            scan(oo[0:32, h, 9:78], T.eg[0:32, MUL + a:MUL + a + 32 * 69:32], T.eg[0:32, ADD + a:ADD + a + 32 * 69:32], "eg" + H, "o00" + H)
         elif c == "f":
             bank, q = BANK[[[1, 2, 3, 5], [6, 7, 0, 4]][h][k]], ("qx", "qn")[h]
             mm(bank, 256, T.qe[:, half(k)], T.qes[:, half(k)], T[q + ts][:], T[q + "s" + ts][:],
@@ -250,18 +260,13 @@ def rank_program(g, core, T, topo):
             vt(T.gm[:, half(h)], T.tab[:].indirect(lst), T.pg[:, half(h)], A.mult, TAB + "pg%d %s" % (h, lk), "gm" + H)
         elif c == "t":
             turn(T.tb[:, half(h)], T.gm[:, half(h)], "gm" + H, "tb" + H)
-        elif c == "d":
-            vt(d1[:, 168 * h + 10 + 2 * k:168 * h + 168:L], T.tb[:, a + k:a + 128:16], T.tb[:, a + 8 + k:a + 128:16], A.add,
-               "d1a d1b tb" + H, "d%d%d" % (h, k))
-        elif c == "D":
-            ac(d1[:, 168 * h + 18:168 * h + 168:L], T.tb[:, a + 12:a + 128:16], "d1a d1b tb" + H, "d%d4" % h)
         elif c == "j":
-            vt(d1[:, 10 + 2 * k:336:L], T.tb[:, k:256:16], T.tb[:, 8 + k:256:16], A.add, "d1a d1b tb0 tb1", "d0%d d1%d" % (k, k))
+            vt(d1[:, 10 + 2 * k:336:L], T.tb[:, k:256:16], T.tb[:, 8 + k:256:16], A.subtract, "d1a d1b tb0 tb1", "d%d" % k)
         elif c == "J":
-            ac(d1[:, 18:336:L], T.tb[:, 12:256:16], "d1a d1b tb0 tb1", "d04 d14")
+            ac(d1[:, 18:336:L], T.tb[:, 12:256:16], "d1a d1b tb0 tb1", "d4")
         elif c == "s":
             q, x = k // 2, k % 2
-            D, a = "oop d1a d1b " + " ".join("d%d%d" % (h, j) for j in range(5)), 168 * h + L * x
+            D, a = "oop d1a d1b d0 d1 d2 d3 d4", 168 * h + L * x
             if k == 7:
                 scan(oo[:, 4 + h, 5:78], oo[:, 2 + h, 10:83], d1[:, a + 10:a + 156:2], D + "".join(" o%d1%d" % (j, h) for j in range(4)), "of" + H)
             else:
@@ -326,7 +331,7 @@ def rank_program(g, core, T, topo):
             dmas("doa", [("y", T.oa[:], T.oaf[0:128:16, :])], "oa0 oa1", "")
 
     for t in range(R):
-        for name in " ".join((CARRY if t else FIRST, STATE, NEXT if t < R - 1 else LAST)).split():
+        for name in " ".join((SIGNS if t else FIRST, CARRY, STATE, NEXT if t < R - 1 else LAST)).split():
             step(t, name)
     for s in sorted(cnt):
         if known["g"].get(s, 0) < cnt[s]:

@@ -8,11 +8,11 @@ BIG = 1.5 * 2.0 ** 23
 SCRATCH = {}
 for _d, _l in (
         ("int32", "nxi:128 yy:16,5,2 ali:16"),
-        ("float32", "uu:16,5,16 tab:256 cs:10,16 ct:10,16 am:16 pat:8,21 i16:8 d1:360 ini:168 oo:6,84 pg:256 gm:256 tb:256 "
-                    "t1:2,2,32 t2l:2,2,16 t2h:2,2,16 t3:2,64 idt:256 oaf:256 ys:256"),
+        ("float32", "uu:16,5,16 tab:256 cs:10,16 ct:10,16 am:16 pat:8,21 i16:8 d1:360 ini:168 oo:4,84 pg:256 gm:256 tb:256 "
+                    "idt:256 oaf:256 ys:256"),
         ("bfloat16", "i64:128 c64:128 et:516 ut:512 vt:512 sb:256 eg:6112 fl:1024 fh:1024 x0:1024 "
                      "xl1:512 xl2:512 xl3:512 xh1:512 xh2:512 xh3:512 zl0:512 zl1:512 zl2:512 zh0:512 zh1:512 zh2:512"),
-        ("uint16", "ul:8 g0:16 gl0:8 gl1:8 gl2:8 go0:8 go1:8 go2:8 ga0:8 ga1:8 ga2:8")):
+        ("uint16", "ul:8 g0:16 nn:4,672 t2l:2,2,16 t2h:2,2,16 gl0:64 gl1:64 gl2:64 go0:64 go1:64 go2:64 ga0:8 ga1:8 ga2:8")):
     for _s in _l.split():
         SCRATCH[_s.split(":")[0]] = ("sbuf", [128] + [int(k) for k in _s.split(":")[1].split(",")], _d)
 for _s in "qe:512 lw:512 qu:128 qy:128 qv:128 qx:256:4 qh:128:3 ql:128:3 qn:256:3".split():
@@ -25,9 +25,11 @@ for _s in BANK:
     SCRATCH[_s] = ("psum", [128, 512], "float32")
 SEMAPHORES = ("cv cs ct cg dnx dal dx du dv dw dyl dyh doa docl doch".split()
               + [n + "%d" % t for n in ("rc", "lc", "rs", "ls", "rg", "lg") for t in range(R)])
-FIRST = "bH TL0 TL1 bL GH GL TL2 TL3 eH EL1 eL EL2 PH PL fL0 fL1 tH iH tL iL JL jL0 jL1 jL2 jL3 EL3 fL2"
+FIRST = ("EL0 AL AH UL lL1 KL lL2 0L 0H SL ML MH lL3 lL4 bL CL bH TL0 TL1 GH TL2 TL3 eH EL1 GL eL "
+         "PH PL fL0 tH tL iL iH JL jL0 jL1 jL2 jL3 EL2 fL1 fL2")
 SIGNS = "bH iL pH pL fL0 fL1 fL2 tH eH tL JL iH jL0 jL1 jL2 jL3"
-CARRY = "fL3 fH0 fH1 fH2 fH3 " + " ".join("sH%d sL%d" % (k, k) for k in range(8)) + " nH nL uH uL vH vL wH wL"
+CARRY = ("sH0 sL0 EL3 fL3 fH0 fH1 fH2 fH3 sH1 sL1 sH2 sL2 NL0 sH3 sL3 sH4 sL4 NL1 sH5 sL5 sH6 sL6 NL2 "
+         "sH7 nH sL7 nL uH uL vH vL")
 STATE = "VL zL0 zL1 zL2 zL3 qL rL0 rL1 rL2 rL3 zH0 zH1 zH2 zH3 qH rH0 rH1 rH2 rH3 XL0 xL1 XL2 xL3 gL QL mL XH0 xH1 XH2 xH3 gH"
 NEXT = "bL QH mH eL"
 LAST = "OL yL QH mH yH"
@@ -164,7 +166,7 @@ def rank_program(g, core, T, topo):
     op("g", lambda: g.affine_select(T.i64[:], T.c64[:], [[-1, 128]], A.is_equal, 0.0, 0, 1), "c64", "i64")
     iota(T.idt[:], [[1, 256]], 0, 0, "idt")
     slots = [(0, 6, 0, 4, 1, 0.0), (0, 2, 4, 12, 1, 0.0), (0, 2, 12, 16, 1, -1e29), (2, 4, 4, 8, 1, 1.0), (2, 4, 8, 12, 1, 0.0),
-             (4, 6, 4, 8, 1, 0.0), (4, 6, 8, 12, 1, 1.0), (2, 6, 12, 16, 1, 0.0), (6, 8, 4, 8, 1, 1.0), (6, 8, 12, 16, 1, 2.0 ** -9)]
+             (4, 6, 4, 8, 1, 0.0), (4, 6, 8, 12, 1, 1.0), (2, 6, 12, 16, 1, 0.0), (6, 8, 4, 8, 1, 1.0), (6, 8, 12, 16, 1, 1.0)]
     slots += [(6, 8, k, 16, 8, 2.0 ** -9 / f) for k, f in enumerate((24, 6, 2, 1))]
     for k, (a, b, c, d, e, val) in enumerate(slots):
         if k % 3:
@@ -174,20 +176,27 @@ def rank_program(g, core, T, topo):
     op("v", lambda: V.tensor_tensor_scan(T.i16[:], T.c64[:, 0:8], T.c64[:, 0:8], -128.0, A.add, A.add), "c64", "i16")
     turn(T.ct[:], cs[:], " ".join("cs%d" % k for k in range(len(slots))) + " r4", "ct")
     fill(T.et[:], 0.0, "et")
+    fill(T.nn[:, :, 9:672:L], 0, "nn")
     const(uu[:, :, 0, 4:8], 64, 0.0, "u0")
-
-    def unpacker(b):
-        quant(T.qe[:, half(b)], T.qes[:, half(b)], T.et[:, 3 - b:515 - b], "et", "qe%d" % b)
-
     for b in range(2):
         vs(T.yy[:, :, 0, b], T.am[:], r4, None, A.add, "am ct", "ua%d" % b)
-    vs(uu[:, :, 0, 12], T.am[:], r4, -128.0, A.add, "am ct", "u12", A.add)
+    vs(uu[:, :, 0, 12], T.am[:], r4, 0.25, A.add, "am ct", "u12", A.add)
     vs(T.ul[:], T.i16[:], 0.125, bit, A.mult, "i16 ct", "ul", A.add)
     const(uu[:, :, 0, 13:16], 48, 0.0, "u1")
-    for a, b, val in ((0, 10, 0.0), (10, 11, BIG), (11, 12, -BIG - 3.0), (12, 20, 1.0), (20, 21, 0.0)):
+    terms = ((0, 10, 0.0), (10, 11, BIG), (11, 12, -BIG - 3.0), (12, 14, 1.0), (14, 15, 512.0), (15, 16, 2.0 ** -9), (16, 19, 1.0),
+             (19, 20, 512.0), (20, 21, 0.0))
+    for a, b, val in terms:
         const(T.pat[:, :, a:b], 8 * (b - a), val, "pat%d" % a)
     ac(T.et[:, 3:515:4], T.i64[:], "i64 et", "et")
-    UA, PAT = "u0 u1 ua0 ua1 ", "pat0 pat10 pat11 pat12 pat20"
+    UA, PAT, TAB = "u0 u1 ua0 ua1 ", " ".join("pat%d" % a for a, _, _ in terms), "tab0 tab1 tab2 tab3 "
+    lists = [(T.g0[:, 0:8], "g0"), (T.g0[:, 8:16], "g0")]
+    vc(T.g0[:], T.ali[:], "ali", "g0")
+    for b in range(2):
+        turn(T.yy[:, :, 1:5, 1 - b], T.nxi[:, 64 * b:64 * b + 64], "nxi", "y%d" % b)
+    ac(T.ini[:], T.pat[:], PAT, "ini")
+    ac(d1[:, 0:336:2], T.pat[:], PAT, "d1a")
+    ac(d1[:, L:L + 336:2], T.pat[:], PAT, "d1b")
+    MUL, ADD, EDGE = 400, 736, 636
 
     def score_mm(t, h):
         mm(BANK[4 * h], 128, T.qy[:], T.qys[:], T["qx%d" % t][:, half(h)], T["qxs%d" % t][:, half(h)], "qy qys qx%d" % t + "LH"[h])
@@ -197,49 +206,41 @@ def rank_program(g, core, T, topo):
         send(T["qn%d" % t][:].bitcast(dt.uint8), T["qx%d" % t][:].bitcast(dt.uint8), "c", t, k, "qnc%d" % t)
         send(T["qns%d" % t][:], T["qxs%d" % t][:], "s", t, k, "qns%d" % t)
 
-    def level(k):
-        src, s = (uu, slice(5 - k, 16, 8)) if k > 1 else (T.yy, slice(0, 2))
-        vt(uu[:, :, 0:5 - k, 4 - k:12:8], src[:, :, 1:6 - k, s], src[:, :, 0:5 - k, s], A.subtract,
-           UA + "y0 y1" if k == 1 else "lv%d" % (k - 1), "lv%d" % k)
-
-    lists = [(T.g0[:, 0:8], "g0"), (T.g0[:, 8:16], "g0")]
-    vc(T.g0[:], T.ali[:], "ali", "g0")
-    for b in range(2):
-        turn(T.yy[:, :, 1:5, 1 - b], T.nxi[:, 64 * b:64 * b + 64], "nxi", "y%d" % b)
-    ac(T.ini[:], T.pat[:], PAT, "ini")
-    ac(d1[:, 0:336:2], T.pat[:], PAT, "d1a")
-    ac(d1[:, L:L + 336:2], T.pat[:], PAT, "d1b")
-    unpacker(0)
-    level(1)
-    quant(T.qu[:], T.qus[:], T.ut[:], "ut", "qu")
-    level(2)
-    vc(T.qy[:].bitcast(dt.uint32), T.qu[:].bitcast(dt.uint32).indirect(T.ul[:]), "qu ul", "qy")
-    ac(T.qys[:], T.qus[:].indirect(T.ul[:]), "qu ul", "qys")
-    MUL, ADD, EDGE = 400, 736, 636
-    ac(T.eg[:, ADD:ADD + 32 * 168:32], T.pat[:], PAT, "ea")
-    ac(T.eg[:, MUL:MUL + 32 * 163:32], T.ini[:, 5:168], "ini", "eb")
-    const(T.eg[:, ADD + 32 * 9:6112:32 * L], 8, 2.0, "ea")
-    const(T.eg[:, ADD + 32 * 11:6112:32 * L], 8, -2.0, "ea ec")
-    const(T.t1[:], 128, 0.0, "t10 t11")
-    const(oo[:, :, 78:83], 30, 1.0, "oop")
-    quant(T.qx0[:, 128:256], T.qxs0[:, 128:256], T.x0[:, 512:1024], "x0", "qx0H")
-    score_mm(0, 1)
-    level(3)
-    quant(T.qx0[:, 0:128], T.qxs0[:, 0:128], T.x0[:, 0:512], "x0", "qx0L")
-    score_mm(0, 0)
-    send_state(0)
-    level(4)
-    TAB = "tab0 tab1 tab2 tab3 "
-
     def step(t, name):
         c, h, k = name[0], "LH".index(name[1]), int(name[2:] or 0)
         ts, H, lh = "%d" % t, "%d" % h, "lh"[h]
         a, bank = 128 * h, BANK[4 * h + k % 4]
         lst, lk = lists[h]
-        if c == "T":
+        if c in "EV" and t:
+            return
+        if c == "E":
+            quant(T.qe[:, half(k)], T.qes[:, half(k)], T.et[:, 3 - k:515 - k], "et", "qe%d" % k)
+        elif c == "A":
+            last = T.yy[quad(3), 4 + 8 * h:8 + 8 * h, 1:5, :]
+            vs(last, last, 511, None, A.bitwise_and, "y0 y1", "ym" + H)
+        elif c == "l":
+            src, s = (uu, slice(5 - k, 16, 8)) if k > 1 else (T.yy, slice(0, 2))
+            vt(uu[:, :, 0:5 - k, 4 - k:12:8], src[:, :, 1:6 - k, s], src[:, :, 0:5 - k, s], A.subtract,
+               UA + "y0 y1 ym0 ym1" if k == 1 else "lv%d" % (k - 1), "lv%d" % k)
+        elif c == "T":
             turn(T.tab[:, k:256:4], uu[:, k:16:4, 0, :], UA + "u12 lv1 lv2 lv3 lv4", "tab%d" % k)
-        elif c == "E":
-            unpacker(k)
+        elif c == "U":
+            quant(T.qu[:], T.qus[:], T.ut[:], "ut", "qu")
+        elif c == "K":
+            vc(T.qy[:].bitcast(dt.uint32), T.qu[:].bitcast(dt.uint32).indirect(T.ul[:]), "qu ul", "qy")
+            ac(T.qys[:], T.qus[:].indirect(T.ul[:]), "qu ul", "qys")
+        elif c == "C":
+            ac(T.eg[:, ADD:ADD + 32 * 168:32], T.pat[:], PAT, "ea")
+            ac(T.eg[:, MUL:MUL + 32 * 163:32], T.ini[:, 5:168], "ini", "eb")
+            const(T.eg[:, ADD + 32 * 9:6112:32 * L], 8, 2.0, "ea")
+            const(T.eg[:, ADD + 32 * 11:6112:32 * L], 8, -2.0, "ea ec")
+            ac(oo[:, :, 78:83], T.pat[:, 0:4, 15:20], PAT, "oop")
+        elif c == "0":
+            quant(T.qx0[:, half(h)], T.qxs0[:, half(h)], T.x0[:, 512 * h:512 * h + 512], "x0", "qx0" + name[1])
+        elif c == "M":
+            score_mm(0, h)
+        elif c == "S":
+            send_state(0)
         elif c == "b":
             vs(T.sb[:, half(h)], T[bank][:, 0:128], thr, less, A.is_gt, "ct " + bank, "sb" + H, A.subtract)
         elif c == "e":
@@ -268,25 +269,25 @@ def rank_program(g, core, T, topo):
             q, x = k // 2, k % 2
             D, a = "oop d1a d1b d0 d1 d2 d3 d4", 168 * h + L * x
             if k == 7:
-                scan(oo[:, 4 + h, 5:78], oo[:, 2 + h, 10:83], d1[:, a + 10:a + 156:2], D + "".join(" o%d1%d" % (j, h) for j in range(4)), "of" + H)
+                scan(T.nn[quad(3), 2 * h + 1, 5:73], oo[quad(3), 2 + h, 10:78], d1[quad(3), a + 10:a + 146:2], D + " nn o31" + H, "n3" + H)
             else:
                 scan(oo[quad(q + x), 2 * (1 - x) + h, 5:78], oo[quad(q), 2 * x + h, 10:83], d1[quad(q), a + 10:a + 156:2],
                      D + " o%d%d%d" % (q, x, h), "o%d%d%d" % (q + x, 1 - x, h))
         elif c == "n":
-            vt(T.t1[:, h, :, 0:4], oo[:, 2 + h:6:2, 9:84:L], oo[:, 2 + h:6:2, 14:84:L], A.subtract,
-               "of" + H + "".join(" o%d1%d" % (j, h) for j in range(4)), "t1" + H)
+            vt(T.nn[:, 2 * h, 9:84:L], oo[:, 2 + h, 9:84:L], oo[:, 2 + h, 14:84:L], A.subtract,
+               "nn" + "".join(" o%d1%d" % (j, h) for j in range(4)), "ne" + H)
+        elif c == "N":
+            vt(T.nn[quad(k), 1:4:2, 9:84:L], oo[quad(k + 1), 0:2, 9:84:L], oo[quad(k + 1), 0:2, 14:84:L], A.subtract,
+               "nn o%d00 o%d01" % (k + 1, k + 1), "n%d0 n%d1" % (k, k))
         elif c == "u":
-            turn(T["t2" + lh][:], T.t1[:, h], "t1" + H, "t2" + H)
+            turn(T["t2" + lh][:], T.nn[:, 2 * h:2 * h + 2, 9:672:L], "ne" + H + "".join(" n%d%d" % (j, h) for j in range(4)), "t2" + H)
         elif c == "v":
             for j in range(2):
-                turn(T.t3[:, h, j:64:2], T["t2" + lh][:, :, j, :], "t2" + H, "t3%d%d" % (h, j))
-        elif c == "w":
-            n = ("gl", "go")[h] + ts
-            vs(T[n][:], T.t3[:, h, 0:8], 512.0, 128.25, A.mult, "t3%d0 t3%d1" % (h, h), n, A.add)
+                turn(T[("gl", "go")[h] + ts][:, j:64:2], T["t2" + lh][:, :, j, :], "t2" + H, "g%d%d%d" % (t, h, j))
+            lists[h] = (T["gl" + ts][:, 0:8], "g%d00 g%d01" % (t, t))
             if h:
-                send(T["ga" + ts][:], T[n][:], "g", t, n, "ga" + ts)
-                n = "ga" + ts
-            lists[h] = (T[n][:], n)
+                send(T["ga" + ts][:], T["go" + ts][:, 0:8], "g", t, "g%d10 g%d11" % (t, t), "ga" + ts)
+                lists[h] = (T["ga" + ts][:], "ga" + ts)
         elif c == "z":
             (vc if k < 2 else ac)(T["z" + lh + ts][:, k:512:4], T["f" + lh][:, 256 * k:256 * k + 256].indirect(lst),
                                   "f%s%d %s" % (lh, k, lk), "z%s%s%d" % (lh, ts, k))
@@ -325,7 +326,7 @@ def rank_program(g, core, T, topo):
                 ac(T.pg[:, half(h)], T.tab[:].indirect(lst), "ct " + TAB + lk, "pg" + H, scl)
             else:
                 ac(T.oaf[:, half(h)], T.idt[:].indirect(lst), "idt " + lk, "oa" + H)
-        elif c == "V" and t == 0:
+        elif c == "V":
             quant(T.qv[:], T.qvs[:], T.vt[:], "vt", "qv")
         elif c == "O":
             dmas("doa", [("y", T.oa[:], T.oaf[0:128:16, :])], "oa0 oa1", "")

from concourse.mybir import dt, AluOpType, ActivationFunctionType

A = AluOpType
AF = ActivationFunctionType
R = 3
L = 21
BIG = 1.5 * 2.0 ** 23
SCRATCH = {}
for _d, _l in (
        ("int32", "nxi:128 yy:16,5,2 ali:16"),
        ("float32", "uu:16,5,16 tab:256 cs:10,16 ct:10,16 am:16 pat:8,21 i16:8 d1:360 ini:168 oo:4,84 pg:256 gm:256 tb:256 "
                    "idt:256 oaf:256 ys:256"),
        ("bfloat16", "i64:128 c64:128 et:516 ut:512 vt:512 sb:256 eg:6112 fl:1024 fh:1024 x0:1024 "
                     "xl1:512 xl2:512 xl3:512 xh1:512 xh2:512 xh3:512 zl0:512 zl1:512 zl2:512 zh0:512 zh1:512 zh2:512"),
        ("uint16", "ul:8 g0:16 nn:4,672 t2l:2,2,16 t2h:2,2,16 gl0:64 gl1:64 gl2:64 go0:64 go1:64 go2:64 ga0:8 ga1:8 ga2:8")):
    for _s in _l.split():
        SCRATCH[_s.split(":")[0]] = ("sbuf", [128] + [int(k) for k in _s.split(":")[1].split(",")], _d)
for _s in "qe:512 lw:512 qu:128 qy:128 qv:128 qx:256:4 qh:128:3 ql:128:3 qn:256:3".split():
    _p = _s.split(":")
    for _t in ([""] if len(_p) == 2 else ["%d" % k for k in range(int(_p[2]))]):
        SCRATCH[_p[0] + _t] = ("sbuf", [128, int(_p[1])], "float8_e4m3fn_x4")
        SCRATCH[_p[0] + "s" + _t] = ("sbuf", [128, int(_p[1])], "uint8")
BANK = ["b%d" % k for k in range(10, 18)]
for _s in BANK:
    SCRATCH[_s] = ("psum", [128, 512], "float32")
SEMAPHORES = ("cv cs ct cg dnx dal dx du dv dw dyl dyh doa docl doch".split()
              + [n + "%d" % t for n in ("rc", "lc", "rs", "ls", "rg", "lg") for t in range(R)])
FIRST = ("EL0 AL AH UL lL1 KL lL2 0L 0H SL ML MH lL3 lL4 bL CL bH TL0 TL1 GH TL2 TL3 eH EL1 GL eL "
         "PH PL fL0 tH tL iL iH JL jL0 jL1 jL2 jL3 EL2 fL1 fL2")
SIGNS = "bH iL pH pL fL0 fL1 fL2 tH eH tL JL iH jL0 jL1 jL2 jL3"
CARRY = ("sH0 sL0 EL3 fL3 fH0 fH1 fH2 fH3 sH1 sL1 sH2 sL2 NL0 sH3 sL3 sH4 sL4 NL1 sH5 sL5 sH6 sL6 NL2 "
         "sH7 nH sL7 nL uH uL vH vL")
STATE = "VL zL0 zL1 zL2 zL3 qL rL0 rL1 rL2 rL3 zH0 zH1 zH2 zH3 qH rH0 rH1 rH2 rH3 XL0 xL1 XL2 xL3 gL QL mL XH0 xH1 XH2 xH3 gH"
NEXT = "bL QH mH eL"
LAST = "OL yL QH mH yH"


def rank_program(g, core, T, topo):
    rank = T.rank_of(core)
    if rank is None:
        return
    nxt = T.cores[(rank + 1) % len(T.cores)]
    rid, pid, _ = topo.addr(nxt)
    mask, neng = topo.mask(core, nxt), len(topo.engines(core, nxt))
    V, S, P = g.vector, g.scalar, g.tensor
    eng = {"v": V, "s": S, "t": P, "g": g, "y": g.sync}
    csem = {"v": "cv", "s": "cs", "t": "ct", "g": "cg"}
    cnt, wr, rd = {}, {}, {}
    known = {q: {} for q in eng}

    def deps(q, r, w):
        toks = [wr[k] for k in r if k in wr]
        for k in w:
            toks += rd.get(k, []) + ([wr[k]] if k in wr else [])
        toks = [t for t in toks if known[q].get(t[0], 0) < t[1]]
        best = {}
        for t in toks:
            if t[0] not in best or best[t[0]][1] < t[1]:
                best[t[0]] = t
        for t in list(best.values()):
            if not any(o is not t and o[2].get(t[0], 0) >= t[1] for o in best.values()):
                eng[q].wait_ge(T.sem[t[0]], t[1])
        for t in toks:
            for s, n in list(t[2].items()) + [(t[0], t[1])]:
                known[q][s] = max(known[q].get(s, 0), n)

    def note(tok, r, w):
        for k in r:
            rd.setdefault(k, []).append(tok)
        for k in w:
            wr[k] = tok
            rd[k] = []

    def op(q, fn, r, w, more=""):
        r, w = r.split(), w.split()
        w = w + [k for k in r if k in BANK]
        w = w + ["pool"] * (q == "g")
        deps(q, r, w)
        s = csem[q]
        cnt[s] = cnt.get(s, 0) + 1
        fn().then_inc(T.sem[s], 1)
        clk = dict(known[q])
        clk[s] = cnt[s]
        note((s, cnt[s], clk), r, w + more.split())

    def dmas(sem, lst, r, w):
        r, w = r.split(), w.split()
        qs = sorted(set(q for q, _, _ in lst))
        for q in qs:
            deps(q, r, w)
        for q, o, i in lst:
            cnt[sem] = cnt.get(sem, 0) + 16
            eng[q].dma_start(o, i).then_inc(T.sem[sem], 16)
        clk = {sem: cnt[sem]}
        for q in qs:
            for s, n in known[q].items():
                clk[s] = max(clk.get(s, 0), n)
        note((sem, cnt[sem], clk), r, w)

    def send(out, inp, k, t, r, lands):
        rs, ls, r = "r%s%d" % (k, t), "l%s%d" % (k, t), r.split()
        deps("g", r, [])
        g.remote_dma(out, inp, T.sem[rs], T.sem[ls], pid, rid, mask)
        for s in (ls, rs):
            cnt[s] = cnt.get(s, 0) + neng
        note((ls, cnt[ls], {}), r, [])
        note((rs, cnt[rs], {}), [], [lands])

    def vs(out, i, s1, s2, o1, r, w, o2=None):
        if o2 is None:
            op("v", lambda: V.tensor_scalar(out, i, s1, None, o1), r, w)
        else:
            op("v", lambda: V.tensor_scalar(out, i, s1, s2, o1, o2), r, w)

    def vt(out, a, b, o, r, w):
        op("v", lambda: V.tensor_tensor(out, a, b, o), r, w)

    def vc(out, i, r, w):
        op("v", lambda: V.tensor_copy(out, i), r, w)

    def ac(out, i, r, w, scale=None):
        if scale is None:
            op("s", lambda: S.activation(out, i, AF.Copy), r, w)
        else:
            op("s", lambda: S.activation(out, i, AF.Copy, scale=scale), r, w)

    def fill(ap, c, w):
        op("v", lambda: V.memset(ap, c), "", w)

    def const(ap, n, c, w):
        ac(ap, T.c64[:, 0:n], "c64", w, c / 64.0)

    def quant(o, s, i, r, w):
        op("v", lambda: V.quantize_mx(o, s, i), r, w)

    def turn(o, i, r, w):
        op("v", lambda: V.transpose(o, i), r, w)

    def scan(o, d0, d1, r, w):
        op("v", lambda: V.tensor_tensor_scan(o, d0, d1, 0.0, A.mult, A.add), r, w)

    def iota(o, pat, base, cm, w, r=""):
        op("g", lambda: g.iota(o, pat, base, cm, allow_small_or_imprecise_dtypes=True), r, w)

    def mm(bank, n, l, ls, rh, rs, r, start=True, stop=True):
        op("t", lambda: P.matmul_mx(T[bank][:, 0:n], l, ls, rh, rs, start, stop), r, bank if start else "", bank)

    def half(h):
        return slice(128 * h, 128 * h + 128)

    def quad(q):
        return slice(32 * q, 32 * q + 32)

    uu, cs, d1, oo = T.uu, T.cs, T.d1, T.oo
    thr, bit, less, scl, r4 = [T.ct[:, 2 * k, 0:1] for k in range(5)]
    dmas("dnx", [("y", T.nxi[:], T.nx[:])], "", "nxi")
    dmas("dal", [("s", T.ali[:], T.al[:])], "", "ali")
    dmas("du", [("y", T.ut[:], T.u[:])], "", "ut")
    dmas("dx", [("y", T.x0[:], T.x[:])], "", "x0")
    dmas("dw", [("y", T.lw[:].bitcast(dt.uint8), T.wc[:]), ("y", T.lws[:], T.ws[:])], "x0", "lw")
    dmas("dv", [("y", T.vt[:], T.v[:])], "", "vt")

    fill(T.c64[:], 64.0, "c64")
    iota(cs[:, 8:10, :], [[4, 32]], 0, 0, "r4")
    iota(T.am[:], [[128, 2], [0, 2], [1, 4]], 0, 0, "am")
    op("g", lambda: g.affine_select(T.i64[:], T.c64[:], [[-1, 128]], A.is_equal, 0.0, 0, 1), "c64", "i64")
    iota(T.idt[:], [[1, 256]], 0, 0, "idt")
    slots = [(0, 6, 0, 4, 1, 0.0), (0, 2, 4, 12, 1, 0.0), (0, 2, 12, 16, 1, -1e29), (2, 4, 4, 8, 1, 1.0), (2, 4, 8, 12, 1, 0.0),
             (4, 6, 4, 8, 1, 0.0), (4, 6, 8, 12, 1, 1.0), (2, 6, 12, 16, 1, 0.0), (6, 8, 4, 8, 1, 1.0), (6, 8, 12, 16, 1, 1.0)]
    slots += [(6, 8, k, 16, 8, 2.0 ** -9 / f) for k, f in enumerate((24, 6, 2, 1))]
    for k, (a, b, c, d, e, val) in enumerate(slots):
        if k % 3:
            fill(cs[:, a:b, c:d:e], val, "cs%d" % k)
        else:
            const(cs[:, a:b, c:d:e], (b - a) * len(range(c, d, e)), val, "cs%d" % k)
    op("v", lambda: V.tensor_tensor_scan(T.i16[:], T.c64[:, 0:8], T.c64[:, 0:8], -128.0, A.add, A.add), "c64", "i16")
    turn(T.ct[:], cs[:], " ".join("cs%d" % k for k in range(len(slots))) + " r4", "ct")
    fill(T.et[:], 0.0, "et")
    fill(T.nn[:, :, 9:672:L], 0, "nn")
    const(uu[:, :, 0, 4:8], 64, 0.0, "u0")
    for b in range(2):
        vs(T.yy[:, :, 0, b], T.am[:], r4, None, A.add, "am ct", "ua%d" % b)
    vs(uu[:, :, 0, 12], T.am[:], r4, 0.25, A.add, "am ct", "u12", A.add)
    vs(T.ul[:], T.i16[:], 0.125, bit, A.mult, "i16 ct", "ul", A.add)
    const(uu[:, :, 0, 13:16], 48, 0.0, "u1")
    terms = ((0, 10, 0.0), (10, 11, BIG), (11, 12, -BIG - 3.0), (12, 14, 1.0), (14, 15, 512.0), (15, 16, 2.0 ** -9), (16, 19, 1.0),
             (19, 20, 512.0), (20, 21, 0.0))
    for a, b, val in terms:
        const(T.pat[:, :, a:b], 8 * (b - a), val, "pat%d" % a)
    ac(T.et[:, 3:515:4], T.i64[:], "i64 et", "et")
    UA, PAT, TAB = "u0 u1 ua0 ua1 ", " ".join("pat%d" % a for a, _, _ in terms), "tab0 tab1 tab2 tab3 "
    lists = [(T.g0[:, 0:8], "g0"), (T.g0[:, 8:16], "g0")]
    vc(T.g0[:], T.ali[:], "ali", "g0")
    for b in range(2):
        turn(T.yy[:, :, 1:5, 1 - b], T.nxi[:, 64 * b:64 * b + 64], "nxi", "y%d" % b)
    ac(T.ini[:], T.pat[:], PAT, "ini")
    ac(d1[:, 0:336:2], T.pat[:], PAT, "d1a")
    ac(d1[:, L:L + 336:2], T.pat[:], PAT, "d1b")
    MUL, ADD, EDGE = 400, 736, 636

    def score_mm(t, h):
        mm(BANK[4 * h], 128, T.qy[:], T.qys[:], T["qx%d" % t][:, half(h)], T["qxs%d" % t][:, half(h)], "qy qys qx%d" % t + "LH"[h])

    def send_state(t):
        k = "qx%dL qx%dH" % (t, t)
        send(T["qn%d" % t][:].bitcast(dt.uint8), T["qx%d" % t][:].bitcast(dt.uint8), "c", t, k, "qnc%d" % t)
        send(T["qns%d" % t][:], T["qxs%d" % t][:], "s", t, k, "qns%d" % t)

    def step(t, name):
        c, h, k = name[0], "LH".index(name[1]), int(name[2:] or 0)
        ts, H, lh = "%d" % t, "%d" % h, "lh"[h]
        a, bank = 128 * h, BANK[4 * h + k % 4]
        lst, lk = lists[h]
        if c in "EV" and t:
            return
        if c == "E":
            quant(T.qe[:, half(k)], T.qes[:, half(k)], T.et[:, 3 - k:515 - k], "et", "qe%d" % k)
        elif c == "A":
            last = T.yy[quad(3), 4 + 8 * h:8 + 8 * h, 1:5, :]
            vs(last, last, 511, None, A.bitwise_and, "y0 y1", "ym" + H)
        elif c == "l":
            src, s = (uu, slice(5 - k, 16, 8)) if k > 1 else (T.yy, slice(0, 2))
            vt(uu[:, :, 0:5 - k, 4 - k:12:8], src[:, :, 1:6 - k, s], src[:, :, 0:5 - k, s], A.subtract,
               UA + "y0 y1 ym0 ym1" if k == 1 else "lv%d" % (k - 1), "lv%d" % k)
        elif c == "T":
            turn(T.tab[:, k:256:4], uu[:, k:16:4, 0, :], UA + "u12 lv1 lv2 lv3 lv4", "tab%d" % k)
        elif c == "U":
            quant(T.qu[:], T.qus[:], T.ut[:], "ut", "qu")
        elif c == "K":
            vc(T.qy[:].bitcast(dt.uint32), T.qu[:].bitcast(dt.uint32).indirect(T.ul[:]), "qu ul", "qy")
            ac(T.qys[:], T.qus[:].indirect(T.ul[:]), "qu ul", "qys")
        elif c == "C":
            ac(T.eg[:, ADD:ADD + 32 * 168:32], T.pat[:], PAT, "ea")
            ac(T.eg[:, MUL:MUL + 32 * 163:32], T.ini[:, 5:168], "ini", "eb")
            const(T.eg[:, ADD + 32 * 9:6112:32 * L], 8, 2.0, "ea")
            const(T.eg[:, ADD + 32 * 11:6112:32 * L], 8, -2.0, "ea ec")
            ac(oo[:, :, 78:83], T.pat[:, 0:4, 15:20], PAT, "oop")
        elif c == "0":
            quant(T.qx0[:, half(h)], T.qxs0[:, half(h)], T.x0[:, 512 * h:512 * h + 512], "x0", "qx0" + name[1])
        elif c == "M":
            score_mm(0, h)
        elif c == "S":
            send_state(0)
        elif c == "b":
            vs(T.sb[:, half(h)], T[bank][:, 0:128], thr, less, A.is_gt, "ct " + bank, "sb" + H, A.subtract)
        elif c == "e":
            turn(T.eg[0:32, EDGE + L * a:EDGE + L * (a + 128):L], T.sb[0:32, half(h)], "ea eb ec sb" + H, "eg" + H)
        elif c == "i":
            a = L * a + 32 * 9
            scan(oo[0:32, h, 9:78], T.eg[0:32, MUL + a:MUL + a + 32 * 69:32], T.eg[0:32, ADD + a:ADD + a + 32 * 69:32], "eg" + H, "o00" + H)
        elif c == "f":
            bank, q = BANK[[[1, 2, 3, 5], [6, 7, 0, 4]][h][k]], ("qx", "qn")[h]
            mm(bank, 256, T.qe[:, half(k)], T.qes[:, half(k)], T[q + ts][:], T[q + "s" + ts][:],
               "qe%d " % k + ("qx%sL qx%sH", "qnc%s qns%s")[h] % (ts, ts))
            ac(T["f" + lh][:, 256 * k:256 * k + 256], T[bank][:, 0:256], bank, "f%s%d" % (lh, k), 0.015625)
        elif c == "p":
            vt(T.gm[:, half(h)], T.sb[:].indirect(lst), T.pg[:, half(h)], A.mult, "sb0 sb1 pg%d %s" % (h, lk), "gm" + H)
        elif c == "G":
            ac(T.pg[:, half(h)], T.sb[:].indirect(lst), "ct sb0 sb1 " + lk, "pg" + H, scl)
        elif c == "P":
            vt(T.gm[:, half(h)], T.tab[:].indirect(lst), T.pg[:, half(h)], A.mult, TAB + "pg%d %s" % (h, lk), "gm" + H)
        elif c == "t":
            turn(T.tb[:, half(h)], T.gm[:, half(h)], "gm" + H, "tb" + H)
        elif c == "j":
            vt(d1[:, 10 + 2 * k:336:L], T.tb[:, k:256:16], T.tb[:, 8 + k:256:16], A.subtract, "d1a d1b tb0 tb1", "d%d" % k)
        elif c == "J":
            ac(d1[:, 18:336:L], T.tb[:, 12:256:16], "d1a d1b tb0 tb1", "d4")
        elif c == "s":
            q, x = k // 2, k % 2
            D, a = "oop d1a d1b d0 d1 d2 d3 d4", 168 * h + L * x
            if k == 7:
                scan(T.nn[quad(3), 2 * h + 1, 5:73], oo[quad(3), 2 + h, 10:78], d1[quad(3), a + 10:a + 146:2], D + " nn o31" + H, "n3" + H)
            else:
                scan(oo[quad(q + x), 2 * (1 - x) + h, 5:78], oo[quad(q), 2 * x + h, 10:83], d1[quad(q), a + 10:a + 156:2],
                     D + " o%d%d%d" % (q, x, h), "o%d%d%d" % (q + x, 1 - x, h))
        elif c == "n":
            vt(T.nn[:, 2 * h, 9:84:L], oo[:, 2 + h, 9:84:L], oo[:, 2 + h, 14:84:L], A.subtract,
               "nn" + "".join(" o%d1%d" % (j, h) for j in range(4)), "ne" + H)
        elif c == "N":
            vt(T.nn[quad(k), 1:4:2, 9:84:L], oo[quad(k + 1), 0:2, 9:84:L], oo[quad(k + 1), 0:2, 14:84:L], A.subtract,
               "nn o%d00 o%d01" % (k + 1, k + 1), "n%d0 n%d1" % (k, k))
        elif c == "u":
            turn(T["t2" + lh][:], T.nn[:, 2 * h:2 * h + 2, 9:672:L], "ne" + H + "".join(" n%d%d" % (j, h) for j in range(4)), "t2" + H)
        elif c == "v":
            for j in range(2):
                turn(T[("gl", "go")[h] + ts][:, j:64:2], T["t2" + lh][:, :, j, :], "t2" + H, "g%d%d%d" % (t, h, j))
            lists[h] = (T["gl" + ts][:, 0:8], "g%d00 g%d01" % (t, t))
            if h:
                send(T["ga" + ts][:], T["go" + ts][:, 0:8], "g", t, "g%d10 g%d11" % (t, t), "ga" + ts)
                lists[h] = (T["ga" + ts][:], "ga" + ts)
        elif c == "z":
            (vc if k < 2 else ac)(T["z" + lh + ts][:, k:512:4], T["f" + lh][:, 256 * k:256 * k + 256].indirect(lst),
                                  "f%s%d %s" % (lh, k, lk), "z%s%s%d" % (lh, ts, k))
        elif c == "q":
            quant(T["q" + lh + ts][:], T["q" + lh + "s" + ts][:], T["z" + lh + ts][:], " ".join("z%s%s%d" % (lh, ts, j) for j in range(4)), "q" + lh + ts)
        elif c == "r":
            q, qs = T["q" + lh + ts], T["q" + lh + "s" + ts]
            mm(bank, 128, T.lw[:, half(k)], T.lws[:, half(k)], q[:], qs[:], "lw q" + lh + ts, True, False)
            mm(bank, 128, T.qe[:, half(k)], T.qes[:, half(k)], q[:], qs[:], "qe%d q" % k + lh + ts, False, True)
        elif c in "xX":
            xk = "x%s%d" % (lh, t + 1)
            if c == "x":
                vs(T[xk][:, k:512:4], T[bank][:, 0:128], 0.015625, None, A.mult, bank, "%s_%d" % (xk, k))
            else:
                ac(T[xk][:, k:512:4], T[bank][:, 0:128], bank, "%s_%d" % (xk, k), 0.015625)
        elif c == "Q":
            xk, key = "x%s%d" % (lh, t + 1), "qx%d%s" % (t + 1, name[1])
            qn, qns = T["qx%d" % (t + 1)][:, half(h)], T["qxs%d" % (t + 1)]
            quant(qn, qns[:, half(h)], T[xk][:], " ".join("%s_%d" % (xk, b) for b in range(4)), key)
            if t < R - 1 and h:
                send_state(t + 1)
            if t == R - 1:
                out = [("y", T.oc[:, 512 * h:512 * h + 512], qn.bitcast(dt.uint8))]
                out += [("ys"[h * (j // 2)], T.osc[4 * j:4 * j + 4, half(h)], qns[32 * j:32 * j + 4, half(h)]) for j in range(4)]
                dmas("doc" + lh, out, key, "")
        elif c == "m":
            if t < R - 1:
                score_mm(t + 1, h)
            else:
                mm(bank, 128, T.qv[:], T.qvs[:], T.qx3[:, half(h)], T.qxs3[:, half(h)], "qv qx3" + name[1])
        elif c == "y":
            (vc if h else ac)(T.ys[:, half(h)], T[bank][:, 0:128], bank, "ys" + H)
            dmas("dy" + lh, [("s", T.y[:, half(h)], T.ys[:, half(h)])], "ys" + H, "")
        elif c == "g":
            if t < R - 1:
                ac(T.pg[:, half(h)], T.tab[:].indirect(lst), "ct " + TAB + lk, "pg" + H, scl)
            else:
                ac(T.oaf[:, half(h)], T.idt[:].indirect(lst), "idt " + lk, "oa" + H)
        elif c == "V":
            quant(T.qv[:], T.qvs[:], T.vt[:], "vt", "qv")
        elif c == "O":
            dmas("doa", [("y", T.oa[:], T.oaf[0:128:16, :])], "oa0 oa1", "")

    for t in range(R):
        for name in " ".join((SIGNS if t else FIRST, CARRY, STATE, NEXT if t < R - 1 else LAST)).split():
            step(t, name)
    for s in sorted(cnt):
        if known["g"].get(s, 0) < cnt[s]:
            g.wait_ge(T.sem[s], cnt[s])
